import numpy as np, ml_dtypes
CORES = [242,247,114,119]
N = 4
BF = ml_dtypes.bfloat16
def gentries(a):
    return np.ascontiguousarray(a.reshape(8, 16, -1).transpose(0, 2, 1)).reshape(8, -1)
def gtable(e):
    e = np.asarray(e); return np.ascontiguousarray(e.reshape(8, -1, 16).transpose(0, 2, 1)).reshape(128, -1).astype(np.int32)
F, STEP, CAPP, V, R, D = 2048, 128, 160, 4096, 2, 3
def aim(rng, s):
    p = rng.integers(1, 64, F); o = rng.permutation(F); k = s - int(np.sum(p)); room = (63 - p if k > 0 else p - 1)[o]
    p[o] += np.sign(k) * np.clip(abs(k) - (np.add.accumulate(room) - room), 0, room)
    return p
def rise(rng):
    top = N * CAPP * STEP + int(rng.integers(62, STEP + 1)); lo, hi, best = F, N * CAPP * STEP, -1
    for k in range(20):
        s = (lo + hi) // 2 if k else F; v = aim(rng, s); z = v.copy()
        for a in range(R - 1):
            z[np.flatnonzero(np.diff(np.add.accumulate(z) // STEP, prepend=0))] = 63
        u = int(np.sum(z))
        if u >= top: hi = s
        else:
            lo = s
            if u > best: best, p, last = u, v, z
    total = np.concatenate([np.zeros(1, np.int64), np.add.accumulate(last)]) + 63 * (F - np.arange(F + 1))
    p[np.flatnonzero(total < top)[0]:] = 63
    return p
def links(rng):
    lab = rng.integers(0, rng.integers(8, 257), F); o = np.argsort(lab, kind="stable"); b, c = o[:-1], o[1:]
    on = (lab[b] == lab[c]) & (rng.random(F - 1) > 0.05); v = np.stack([np.arange(F), np.arange(F)])
    v[0, c[on]] = b[on]; v[1, b[on]] = c[on]
    return v
def whole(rng, m, *shape):
    return rng.integers(-m, m + 1, shape).astype(np.float32).astype(BF)
def draw(rng, lo, hi):
    v = np.stack([np.stack([links(rng) for g in range(8)]) for r in range(N)]).astype(np.int32)
    return {"x": whole(rng, 8, N, 128, F), "prv": np.ascontiguousarray(v[:, :, 0]), "nxt": np.ascontiguousarray(v[:, :, 1]), "key": rng.integers(0, V, (N, 8, F)).astype(np.int32), "rw": rng.integers(-255, 256, (N, 8, F)).astype(np.int32),
            "pri": np.stack([gtable(np.stack([aim(rng, int(rng.integers(lo * F, hi * F))) for g in range(8)])) for r in range(N)]), "w": whole(rng, 4, N, 128, 2 * D + 1), "val": whole(rng, 8, N, 128, V)}
def put(d, r, g, p):
    e = gentries(d["pri"][r]); e[g] = p; d["pri"][r] = gtable(e)
def setup_inputs(rng):
    return draw(rng, 24, 34)
def setup_inputs_full(rng):
    d = draw(rng, 24, 34); o = rng.permutation(N); late = rng.random((N, 8)) < 0.2; late[o[1], rng.permutation(8)[:4]] = True; late[o[0]] = False
    m = rng.random((N, 8)) < 0.3; m[o[0]] = True; m = m & ~late
    for r, g in np.argwhere(m):
        put(d, r, g, aim(rng, N * CAPP * STEP + int(rng.integers(0, STEP))))
        d["x"][r, 16 * g:16 * g + 16] = whole(rng, 1, 16, F); d["rw"][r, g] = rng.integers(-60, 61, F)
    for r, g in np.argwhere(late):
        put(d, r, g, rise(rng))
        d["x"][r, 16 * g:16 * g + 16] = 0; d["rw"][r, g] = 340; d["rw"][r, g, 0] = 0
    return d
def setup_inputs_even(rng):
    d = draw(rng, 24, 34)
    for r in range(N):
        d["pri"][r] = gtable(np.repeat(rng.permutation(np.array([16, 16, 16, 32, 32, 32, 32, 32]))[:, None], F, 1))
    return d
def setup_inputs_few(rng):
    d = draw(rng, 24, 34)
    for r in range(N):
        o = rng.permutation(8)[:4]
        for g in o[1:]: d["x"][r, 16 * g:16 * g + 16] = 0
        for g in o[:2]: put(d, r, g, np.ones(F, np.int64))
        for g in o[2:]: put(d, r, g, aim(rng, int(rng.integers(12 * F, 17 * F))))
        d["rw"][r, o[1]] = 0; d["rw"][r, o[2]] = rng.choice(np.array([0, 8, -8, 16, -16, 5, -5]), F); d["rw"][r, o[3]] = rng.choice(np.array([-336, -342, 336, 341, 335, 330]), F)
    return d
def setup_inputs_loose(rng):
    d = draw(rng, 8, 17); d["prv"] = rng.integers(0, F, (N, 8, F)).astype(np.int32); d["nxt"] = rng.integers(0, F, (N, 8, F)).astype(np.int32)
    for n, m in (("x", 8), ("w", 4), ("val", 8)):
        d[n] = (m * (2 * rng.integers(0, 2, d[n].shape) - 1)).astype(np.float32).astype(BF)
    d["rw"] = (1023 * rng.integers(-1, 2, (N, 8, F))).astype(np.int32)
    for r in range(N):
        o = rng.permutation(8)
        d["prv"][r, o[0]] = 0; d["nxt"][r, o[0]] = F - 1; d["prv"][r, o[1]] = np.arange(F); d["nxt"][r, o[1]] = np.arange(F)
        d["prv"][r, o[2]] = (np.arange(F) - 1) % F; d["nxt"][r, o[2]] = (np.arange(F) + 1) % F
        d["key"][r, o[3]] = V - 1; d["key"][r, o[4]] = rng.choice(np.array([0, V - 1]), F)
        d["x"][r, 16 * o[5]:16 * o[5] + 16] = 8
    q = rng.integers(0, N); d["w"][q] = 4; d["val"][q] = 8
    return d
def setup_inputs_spread(rng):
    d = draw(rng, 8, 17)
    for n, m in (("x", F), ("val", V)):
        s = np.left_shift(1, rng.integers(0, 4, (N, 1, m))) * (rng.random((N, 1, m)) > 0.0625)
        d[n] = (rng.integers(-1, 2, (N, 128, m)) * s).astype(np.float32).astype(BF)
    d["w"] = (rng.integers(-4, 5, (N, 128, 2 * D + 1)) * (rng.random((N, 128, 1)) > 0.4)).astype(np.float32).astype(BF)
    d["key"] = np.minimum(rng.random((N, 8, F)) ** 3 * V, V - 1).astype(np.int32)
    d["rw"] = np.right_shift(rng.integers(-1023, 1024, (N, 8, F)), rng.integers(0, 11, (N, 8, F))).astype(np.int32)
    return d
def play(x, prv, nxt, key, rw, pri, w, val):
    X = x.astype(np.float32).reshape(N, 8, 16, F); W = w.astype(np.float32).reshape(N, 8, 16, 2 * D + 1); A = val.astype(np.float32).reshape(N, 8, 16, V)
    P = np.stack([gentries(pri[r]) for r in range(N)]).astype(np.int64); most = 0
    for a in range(R):
        for r in range(N):
            for g in range(8):
                t = np.flatnonzero(np.diff(np.add.accumulate(P[r, g]) // STEP, prepend=0)); most = max(most, len(t))
                q = np.arange(len(t)) % N
                pt = {0: t}
                for k in range(1, D + 1):
                    pt[k] = nxt[r, g][pt[k - 1]]; pt[-k] = prv[r, g][pt[1 - k]]
                h = np.zeros((len(t), 16), np.float32)
                for k in range(-D, D + 1):
                    h += W[q, g, :, D + k] * X[r, g][:, pt[k]].T
                e = np.sum(A[q, g, :, key[r, g][t]] * h, axis=1) + (rw[r, g][pt[0]] + rw[r, g][pt[1]] + rw[r, g][pt[2]])
                P[r, g, t] = np.minimum(np.maximum(np.abs(e).astype(np.int64) >> 4, 1), 63)
    return P, most
def check_inputs(d):
    bad = []
    for n, lo, hi in (("x", -8, 8), ("prv", 0, F - 1), ("nxt", 0, F - 1), ("key", 0, V - 1), ("rw", -1023, 1023), ("pri", 1, 63), ("w", -4, 4), ("val", -8, 8)):
        v = np.asarray(d[n]).astype(np.float32)
        if not (np.isfinite(v).all() and (v == np.floor(v)).all() and v.min() >= lo and v.max() <= hi): bad.append(n)
    if not bad and play(**d)[1] > N * CAPP: bad.append("CAPP")
    return bad
def reference(x, prv, nxt, key, rw, pri, w, val):
    P, most = play(x, prv, nxt, key, rw, pri, w, val)
    y = np.stack([gtable(P[r]) for r in range(N)])
    return {"y": y.astype(np.float32)}

@@ -1,0 +1,370 @@
+from concourse.bass import DstId, RemoteDMATransfer
+from concourse.mybir import dt, AluOpType, AxisListType, ActivationFunctionType
+
+F16, BF, F32, I32, U16 = "float16", "bfloat16", "float32", "int32", "uint16"
+LISTS = ["L0", "L1", "M1", "L2", "M2", "L3", "M3"]
+SCRATCH = {
+    "PRI": ("sbuf", [128, 128], I32), "PB0": ("sbuf", [128, 128], BF), "PB1": ("sbuf", [128, 128], BF),
+    "TI": ("sbuf", [128, 16, 32], I32), "TX": ("sbuf", [128, 16, 32], F16), "TT": ("sbuf", [128, 16, 32], F16),
+    "X": ("sbuf", [128, 2048], BF), "VALB": ("sbuf", [128, 4096], BF), "PW": ("sbuf", [128, 2048], I32),
+    "IM": ("sbuf", [128, 160], I32), "I8": ("sbuf", [128, 128], I32), "KP": ("sbuf", [128, 1], I32), "T8I": ("sbuf", [128, 64], I32),
+    "CI": ("sbuf", [128, 8], I32), "CF": ("sbuf", [128, 8], F32), "CG": ("sbuf", [128, 8], F32),
+    "BO": ("sbuf", [128, 128], BF), "TM": ("sbuf", [128, 128], BF), "ID": ("sbuf", [128, 128], BF), "IDH": ("sbuf", [128, 128], F16),
+    "PM": ("sbuf", [128, 512], F16), "Z2": ("sbuf", [128, 144], F16), "Z2T": ("sbuf", [128, 144], F16), "ZN": ("sbuf", [128, 144], F16),
+    "ZP": ("sbuf", [128, 144], F16), "ES": ("sbuf", [128, 256], F16), "ER": ("sbuf", [128, 256], F16), "T8H": ("sbuf", [128, 64], F16),
+    "ONE": ("sbuf", [128, 128], F32), "CS": ("sbuf", [128, 128], F32), "SI": ("sbuf", [128, 128], I32), "RI": ("sbuf", [128, 128], I32),
+    "K2": ("sbuf", [128, 128], I32), "NF": ("sbuf", [128, 128], F32), "CODE": ("sbuf", [128, 128], F16), "M4": ("sbuf", [128, 512], F16),
+    "MK": ("sbuf", [128, 512], F16), "MN": ("sbuf", [128, 512], F16), "MP": ("sbuf", [128, 512], F16), "RW4": ("sbuf", [128, 512], F16),
+    "KS0": ("sbuf", [128, 64], U16), "KS1": ("sbuf", [128, 64], U16), "KL0": ("sbuf", [128, 64], U16), "KL1": ("sbuf", [128, 64], U16),
+    "VS0": ("sbuf", [128, 1024], BF), "VS1": ("sbuf", [128, 1024], BF), "VR0": ("sbuf", [128, 1024], BF), "VR1": ("sbuf", [128, 1024], BF),
+    "PROD": ("sbuf", [128, 1024], F16), "EM": ("sbuf", [128, 512], F32), "EA": ("sbuf", [128, 256], F32), "EB": ("sbuf", [128, 128], F32),
+    "AB": ("sbuf", [128, 128], F32), "NI": ("sbuf", [128, 128], I32), "NM": ("sbuf", [128, 128], F32), "PK": ("sbuf", [128, 128], F32),
+    "SMP": ("sbuf", [128, 128], F32), "YO": ("sbuf", [128, 128], F32), "WS": ("sbuf", [128, 7], BF), "WF": ("sbuf", [128, 7], F32),
+    "WR": ("sbuf", [128, 32], BF), "WG": ("sbuf", [128, 32], F32), "DG": ("sbuf", [128, 28 * 128], BF),
+    "QA": ("psum", [128, 512], F32), "QB": ("psum", [128, 512], F32), "QT": ("psum", [128, 512], F32), "QE": ("psum", [128, 512], F32),
+}
+for _n in LISTS:
+    SCRATCH[_n] = ("sbuf", [128, 64], U16)
+    SCRATCH["X" + _n] = ("sbuf", [128, 1024], BF)
+for _n in LISTS[1:5]:
+    SCRATCH["R" + _n] = ("sbuf", [128, 1024], F16)
+for _q in range(4):
+    SCRATCH["H%d" % _q] = ("psum", [128, 512], F32)
+SEMAPHORES = (["dpri", "dtab", "dw", "dx", "dval", "dpw", "dy", "gi", "gz", "vc", "vc2", "vc3", "vi8", "ves", "vbo", "vtm", "vtm2", "vpb", "vperm",
+               "vcv", "vtr", "vsel", "vone", "vid", "vscan", "vS", "vr", "vnf", "vcode", "vmsk", "vmk", "vmn", "vmp", "vpk", "eK", "gV", "vrw4", "vdg",
+               "vpr", "vem", "va1", "va2", "vni", "vnm", "vP", "ptab", "pA", "pB", "pK", "ph", "pE", "swf", "sdg", "swg", "sdg2", "sab",
+               "wl", "wr", "kl", "kr0", "kr1", "vl"]
+              + ["e" + n for n in LISTS] + ["p" + n for n in LISTS] + ["s" + n for n in LISTS] + ["g" + n for n in LISTS[1:5]]
+              + ["vr%d_%d" % (a, q) for a in range(2) for q in range(4)])
+
+
+def rank_program(g, core, T, topo):
+    rank = T.rank_of(core)
+    if rank is None:
+        return
+    A = AluOpType
+    COPY, ABS = ActivationFunctionType.Copy, ActivationFunctionType.Abs
+    V, S, P = g.vector, g.scalar, g.tensor
+    Q = {"v": V, "s": S, "t": P, "y": g.sync, "g": g}
+    tot, got = {}, {}
+
+    def done(ins, name, n=1):
+        ins.then_inc(T.sem[name], n)
+        tot[name] = tot.get(name, 0) + n
+
+    def need(q, *names):
+        for n in names:
+            if got.get((q, n), 0) < tot[n]:
+                Q[q].wait_ge(T.sem[n], tot[n])
+                got[(q, n)] = tot[n]
+
+    peers = [c for c in T.cores if c != core]
+
+    def engines_of(src):
+        ps = [c for c in T.cores if c != src]
+        off = [c for c in ps if c not in topo.cores_of(src)]
+        out = {}
+        eo = topo.engines(src, off[0])
+        n = len(eo) // len(off)
+        for k, c in enumerate(off):
+            out[c] = eo[k * n:(k + 1) * n]
+        for c in ps:
+            if c not in out:
+                out[c] = [e for e in topo.engines(src, c) if e not in eo]
+        return out
+
+    eng = engines_of(core)
+    inc = {c: len(engines_of(c)[core]) for c in peers}
+
+    def send(src_of, dst_of, sem_of, local):
+        tr = []
+        for c in peers:
+            rid, pid = topo.addr(c, core)
+            m = 0
+            for e in eng[c]:
+                m |= 1 << e
+            r = T.rank_of(c)
+            tr.append(RemoteDMATransfer(dst_ids=[DstId(rid=rid, pnc=pid)], dma_engine_mask=m, remote_sem=sem_of(r), src=src_of(r), dst=dst_of(r)))
+        g.remote_dma_fused(tr, local_sem=T.sem[local])
+        tot[local] = tot.get(local, 0) + sum(len(eng[c]) for c in peers)
+
+    done(g.sync.dma_start(T.PRI[:], T.pri[:]), "dpri", 16)
+    done(S.dma_start(T.TI[:, 0:4, :], T.key[:]), "dtab", 16)
+    done(g.sync.dma_start(T.TI[:, 4:8, :], T.nxt[:]), "dtab", 16)
+    done(S.dma_start(T.TI[:, 8:12, :], T.prv[:]), "dtab", 16)
+    done(g.sync.dma_start(T.TI[:, 12:16, :], T.rw[:]), "dtab", 16)
+    done(S.dma_start(T.WS[:], T.w[:]), "dw", 16)
+    done(S.dma_start(T.X[:], T.x[:]), "dx", 16)
+
+    done(g.iota(T.IM[:], [[1, 160]], -16, 0), "gi")
+    done(g.iota(T.KP[:], [[0, 1]], 0, 1), "gi")
+    done(g.iota(T.T8I[:], [[0, 4], [128, 16]], 0, 0), "gi")
+    done(g.iota(T.PW[:], [[0, 2048]], 0, 0), "gz")
+    need("y", "gz")
+    done(g.sync.dma_start(T.PW[0:128:16, :], T.nxt[:]), "dpw", 16)
+    done(g.sync.dma_start(T.PW[1:128:16, :], T.prv[:]), "dpw", 16)
+    done(g.sync.dma_start(T.PW[2:128:16, :], T.rw[:]), "dpw", 16)
+    done(g.sync.dma_start(T.VALB[:], T.val[:]), "dval", 16)
+    need("g", "dw")
+    send(lambda r: T.WS[:], lambda r: T.WR[:, 8 * rank:8 * rank + 7], lambda r: T.sem.wr, "wl")
+    tot["wr"] = sum(inc.values())
+
+    need("v", "gi")
+    kp = T.KP[:]
+    m = T.IM[:, 16:144]
+
+    def bits(j, sh, msk):
+        done(V.tensor_scalar(T.CI[:, j:j + 1], kp, sh, msk, A.logical_shift_right, A.bitwise_and), "vc")
+
+    bits(0, 3, 30)
+    bits(1, 0, 15)
+    bits(2, 0, 7)
+    bits(3, 0, 112)
+    bits(4, 3, 1)
+    bits(5, 4, 1)
+    bits(6, 0, 127)
+    bits(7, 0, 127)
+    done(V.tensor_scalar(T.I8[:], m, 3, None, A.logical_shift_right), "vi8")
+    need("v", "vc")
+    done(V.tensor_copy(T.CF[:], T.CI[:]), "vc2")
+    need("v", "vc2", "vi8")
+    cf = lambda j: T.CF[:, j:j + 1]
+    cg = lambda j: T.CG[:, j:j + 1]
+    done(V.tensor_scalar(cg(0), cf(0), 1.0, None, A.add), "vc3")
+    done(V.tensor_tensor(cg(1), cf(3), cf(4), A.add), "vc3")
+    done(V.tensor_scalar(cg(2), cf(1), 0.0, None, A.is_equal), "vc3")
+    done(V.tensor_scalar(cg(3), cf(1), 1.0, None, A.is_equal), "vc3")
+    done(V.tensor_scalar(cg(4), cf(1), 2.0, None, A.is_equal), "vc3")
+    done(V.tensor_scalar(cg(5), cf(5), 0.0, None, A.is_equal), "vc3")
+    done(V.tensor_scalar(cg(6), cf(6), 1.0, None, A.subtract), "vc3")
+    done(V.tensor_scalar(cg(7), cf(1), 8.0, None, A.mult), "vc3")
+    done(V.tensor_scalar(T.TM[:], m, cf(6), -1.0, A.is_lt, A.mult), "vtm")
+    done(V.tensor_scalar(T.ES[:, 0:128], T.I8[:], cf(0), None, A.is_equal), "ves")
+    need("v", "vc3")
+    done(V.tensor_scalar(T.ES[:, 128:256], T.I8[:], cg(0), None, A.is_equal), "ves")
+    need("v", "ves", "vtm")
+    done(V.tensor_tensor(T.BO[:], T.ES[:, 0:128], T.ES[:, 128:256], A.add), "vbo")
+    need("v", "vbo")
+    done(V.tensor_tensor(T.TM[:], T.TM[:], T.BO[:], A.mult), "vtm2")
+    done(V.memset(T.ONE[:], 1.0), "vone")
+    need("v", "dpri")
+    done(V.tensor_copy(T.PB0[:], T.PRI[:]), "vpb")
+    for n, (lo, col, msk) in enumerate([(16, cf(6), cg(5)), (32, cf(6), cf(5)), (0, cf(6), cg(5)), (16, cf(6), cf(5))]):
+        done(V.tensor_scalar(T.PM[:, 128 * n:128 * n + 128], T.IM[:, lo:lo + 128], col, msk, A.is_equal, A.mult), "vperm")
+    need("v", "dtab")
+    done(V.tensor_scalar(T.TX[:, 0:4, :], T.TI[:, 0:4, :], 2048.0, None, A.subtract), "vcv")
+    done(V.tensor_copy(T.TX[:, 4:16, :], T.TI[:, 4:16, :]), "vcv")
+    need("v", "vcv")
+    done(V.transpose(T.TT[:], T.TX[:]), "vtr")
+
+    def sums(a):
+        pb = T.PB0 if a == 0 else T.PB1
+        need("t", "vbo", "vpb" if a == 0 else "vP")
+        done(P.matmul(T.QA[:, 0:128], T.BO[:], pb[:], True, True), "pA")
+        need("t", "vtm2")
+        done(P.matmul(T.QB[:, 0:128], T.TM[:], pb[:], True, True), "pB")
+
+    sums(0)
+    need("t", "vperm", "vtr")
+    for b1 in range(8):
+        bt = b1 % 2
+        for ga in range(2):
+            n = 2 * ga + bt
+            ins = P.matmul(T.QT[:, b1:512:8], T.PM[:, 128 * n:128 * n + 128], T.TT[:, b1 // 2:16:4, 16 * ga:16 * ga + 16], ga == 0, ga == 1)
+        if b1 == 7:
+            done(ins, "ptab")
+
+    done(V.tensor_scalar(T.Z2T[:], T.IM[:, 0:144], cg(1), cf(2), A.is_equal, A.mult), "vsel")
+    done(V.tensor_scalar(T.Z2[:], T.IM[:, 0:144], cg(1), None, A.is_equal), "vsel")
+    done(V.tensor_scalar(T.IDH[:], m, cf(6), None, A.is_equal), "vsel")
+    done(V.tensor_scalar(T.T8H[:], T.T8I[:], cg(7), None, A.add), "vsel")
+    done(V.tensor_scalar(T.ID[:], m, cf(6), None, A.is_equal), "vid")
+
+    need("s", "dw", "vid")
+    done(S.activation(T.WF[:], T.WS[:], COPY), "swf")
+    need("s", "swf")
+    for d in range(7):
+        o = (7 * rank + d) * 128
+        done(S.activation(T.DG[:, o:o + 128], T.ID[:], COPY, scale=T.WF[:, d:d + 1]), "sdg")
+
+    def late_selectors():
+        done(V.tensor_scalar(T.ZN[:], T.IM[:, 0:144], cf(6), cg(2), A.is_equal, A.mult), "vsel")
+        done(V.tensor_scalar(T.ZP[:], T.IM[:, 0:144], cg(6), cg(3), A.is_equal, A.mult), "vsel")
+        done(V.tensor_scalar(T.ER[:, 0:128], T.I8[:], cf(0), cg(4), A.is_equal, A.mult), "vsel")
+        done(V.tensor_scalar(T.ER[:, 128:256], T.I8[:], cg(0), cg(4), A.is_equal, A.mult), "vsel")
+
+    others = [T.rank_of(c) for c in peers]
+    KEYC, NXTC, PRVC, RWC = 0, 128, 256, 384
+    STEP = {"L0": 3, "L1": 4, "L2": 5, "L3": 6, "M1": 2, "M2": 1, "M3": 0}
+
+    def blocksum(name, bank, sel, rows, first=True):
+        for cl in range(8):
+            ins = P.matmul(T[bank][:, 0:64], T[sel][:, 16 - 2 * cl:144 - 2 * cl], T[rows][:, cl:512:8], first and cl == 0, cl == 7)
+        done(ins, name)
+
+    def wrap(lst, bank, sel, rows):
+        for ro in range(16):
+            ins = P.matmul(T[bank][:, 0:64], T[sel][:, 16 - ro:144 - ro], T[rows][:, ro:1024:16], ro == 0, ro == 15)
+        done(ins, "p" + lst)
+
+    def evac(lst, bank):
+        need("v", "p" + lst)
+        done(V.tensor_copy(T[lst][:], T[bank][:, 0:64]), "e" + lst)
+
+    def mul(a, out, col, sem):
+        for q in range(4):
+            done(V.tensor_tensor(T[out][:, 128 * q:128 * q + 128], T.M4[:, 128 * q:128 * q + 128], T.QT[:, col:col + 128], A.mult), sem)
+
+    def pick_x(lst):
+        need("s", "dx", "e" + lst)
+        done(S.activation(T["X" + lst][:], T.X[:].indirect(T[lst][:]), COPY), "s" + lst)
+
+    def pick_p(lst):
+        need("v", "dpw", "e" + lst)
+        done(V.tensor_copy(T["R" + lst][:], T.PW[:].indirect(T[lst][:])), "g" + lst)
+
+    def hsum(lst, k):
+        need("t", "s" + lst)
+        for q in range(4):
+            o = (7 * q + STEP[lst]) * 128
+            ins = P.matmul(T["H%d" % q][:, 0:256], T.DG[:, o:o + 128], T["X" + lst][:, 256 * q:256 * q + 256], k == 0, k == 6)
+            if k == 6:
+                done(ins, "ph")
+
+    def esum(sel, rows, last):
+        for ih in range(2):
+            ins = P.matmul(T.QE[:], T[sel][:, 128 * ih:128 * ih + 128], T[rows][:, ih:1024:2], False, last and ih == 1)
+        if last:
+            done(ins, "pE")
+
+    for a in range(2):
+        pb = T.PB0 if a == 0 else T.PB1
+        KS, KL, VS, VR = T["KS%d" % a], T["KL%d" % a], T["VS%d" % a], T["VR%d" % a]
+        if a:
+            sums(a)
+        need("v", "pA", "vone")
+        done(V.tensor_tensor_scan(T.CS[:], T.ONE[:], T.QA[:, 0:128], 0.0, A.mult, A.add), "vscan")
+        need("v", "pB", "vscan")
+        done(V.tensor_tensor(T.SI[:], T.CS[:], T.QB[:, 0:128], A.add), "vS")
+        need("v", "vS")
+        done(V.tensor_scalar(T.RI[:], T.SI[:], 127, None, A.bitwise_and), "vr")
+        done(V.tensor_scalar(T.K2[:], T.SI[:], 6, 6, A.arith_shift_right, A.bitwise_and), "vr")
+        need("v", "vr")
+        done(V.tensor_tensor(T.NF[:], T.RI[:], pb[:], A.is_ge), "vnf")
+        need("v", "vnf")
+        done(V.tensor_tensor(T.CODE[:], T.K2[:], T.NF[:], A.add), "vcode")
+        need("v", "vcode")
+        for q in range(4):
+            done(V.tensor_scalar(T.M4[:, 128 * q:128 * q + 128], T.CODE[:], float(2 * ((q + 1) % 4)), None, A.is_equal), "vmsk")
+        need("t", "vmsk", "vsel", "vscan")
+        P.matmul(T.QA[:, 0:64], T.IDH[:], T.T8H[:], True, False)
+        blocksum("pL0", "QA", "Z2T", "M4", False)
+        need("v", "vmsk", "ptab")
+        mul(a, "MK", KEYC, "vmk")
+        need("t", "vmk", "vS")
+        blocksum("pK", "QB", "Z2", "MK")
+        evac("L0", "QA")
+        pick_x("L0")
+        mul(a, "MN", NXTC, "vmn")
+        need("t", "vmn", "eL0")
+        blocksum("pL1", "QA", "Z2", "MN")
+        need("v", "pK")
+        done(V.tensor_scalar(KS[:], T.QB[:, 0:64], 2048.0, None, A.add), "eK")
+        done(V.tensor_scalar(KL[:, 16 * rank:16 * rank + 16], T.QB[:, 16 * rank:16 * rank + 16], 2048.0, None, A.add), "eK")
+        kr = "kr%d" % a
+        need("g", "eK")
+        send(lambda r: KS[:, 16 * r:16 * r + 16], lambda r: KL[:, 16 * rank:16 * rank + 16], lambda r: T.sem[kr], "kl")
+        tot[kr] = sum(inc.values())
+        mul(a, "MP", PRVC, "vmp")
+        need("t", "vmp", "eK")
+        blocksum("pM1", "QB", "Z2", "MP")
+        if a == 0:
+            late_selectors()
+        evac("L1", "QA")
+        pick_p("L1")
+        evac("M1", "QB")
+        pick_p("M1")
+        need("t", "vsel", "eL1", "gL1")
+        wrap("L2", "QA", "ZN", "RL1")
+        if a == 0:
+            need("s", "wr")
+            o = others[0]
+            done(S.activation(T.WG[:, 0:7], T.WR[:, 8 * o:8 * o + 7], COPY), "swg")
+            need("s", "swg")
+            for d in range(7):
+                done(S.activation(T.DG[:, (7 * o + d) * 128:(7 * o + d) * 128 + 128], T.ID[:], COPY, scale=T.WG[:, d:d + 1]), "sdg2")
+        pick_x("L1")
+        pick_x("M1")
+        evac("L2", "QA")
+        pick_x("L2")
+        need("t", "eM1", "gM1")
+        wrap("M2", "QB", "ZP", "RM1")
+        if a == 0:
+            for q in range(4):
+                done(V.tensor_copy(T.RW4[:, 128 * q:128 * q + 128], T.QT[:, RWC:RWC + 128]), "vrw4")
+            need("v", "wr", "vid")
+            for o in others[1:]:
+                for d in range(7):
+                    done(V.tensor_scalar(T.DG[:, (7 * o + d) * 128:(7 * o + d) * 128 + 128], T.ID[:], T.WR[:, 8 * o + d:8 * o + d + 1], None, A.mult), "vdg")
+        evac("M2", "QB")
+        pick_x("M2")
+        need("v", "dval", kr, "eK")
+        done(V.tensor_copy(VS[:], T.VALB[:].indirect(KL[:])), "gV")
+        need("g", "gV")
+        send(lambda r: VS[:, 256 * r:256 * r + 256], lambda r: VR[:, 256 * rank:256 * rank + 256], lambda r: T.sem["vr%d_%d" % (a, rank)], "vl")
+        for c in peers:
+            tot["vr%d_%d" % (a, T.rank_of(c))] = inc[c]
+        pick_p("L2")
+        pick_p("M2")
+        need("t", "vrw4")
+        P.matmul(T.QE[:], T.IDH[:], T.RW4[:], True, False)
+        esum("ER", "RL1", False)
+        need("t", "sdg", "sdg2", "vdg")
+        hsum("L0", 0)
+        hsum("L1", 1)
+        hsum("M1", 2)
+        need("t", "eL2", "gL2")
+        wrap("L3", "QA", "ZN", "RL2")
+        evac("L3", "QA")
+        pick_x("L3")
+        hsum("L2", 3)
+        need("t", "eM2", "gM2")
+        wrap("M3", "QB", "ZP", "RM2")
+        evac("M3", "QB")
+        pick_x("M3")
+        done(V.tensor_tensor(T.PK[:], T.NF[:], pb[:], A.mult), "vpk")
+        done(V.tensor_scalar(T.SMP[:], T.NF[:], -1.0, 1.0, A.mult, A.add), "vpk")
+        esum("ER", "RL2", False)
+        hsum("M2", 4)
+        hsum("L3", 5)
+        hsum("M3", 6)
+        need("v", "ph")
+        for q in [rank] + others:
+            if q != rank:
+                need("v", "vr%d_%d" % (a, q))
+            src = VS if q == rank else VR
+            if q == rank:
+                need("v", "gV")
+            done(V.tensor_tensor(T.PROD[:, 256 * q:256 * q + 256], src[:, 256 * q:256 * q + 256], T["H%d" % q][:, 0:256], A.mult), "vpr")
+        need("t", "vpr")
+        esum("ES", "PROD", True)
+        need("v", "pE")
+        done(V.tensor_tensor(T.EM[:], T.M4[:], T.QE[:], A.mult), "vem")
+        need("v", "vem")
+        done(V.tensor_tensor(T.EA[:], T.EM[:, 0:256], T.EM[:, 256:512], A.add), "va1")
+        need("v", "va1")
+        done(V.tensor_tensor(T.EB[:], T.EA[:, 0:128], T.EA[:, 128:256], A.add), "va2")
+        need("s", "va2")
+        done(S.activation(T.AB[:], T.EB[:], ABS, scale=0.0625), "sab")
+        need("v", "sab", "vpk")
+        done(V.tensor_scalar(T.NI[:], T.AB[:], 0.46875, 63.0, A.subtract, A.min), "vni")
+        need("v", "vni")
+        done(V.tensor_tensor(T.NM[:], T.NI[:], T.SMP[:], A.max), "vnm")
+        need("v", "vnm")
+        done(V.tensor_tensor((T.YO if a else T.PB1)[:], T.NM[:], T.PK[:], A.add), "vP")
+    need("y", "vP")
+    done(g.sync.dma_start(T.y[:], T.YO[:]), "dy", 16)
+    need("y", "dy")
+    for n in sorted(tot):
+        if max([got.get((q, n), 0) for q in Q]) < tot[n]:
+            need("g", n)

@@ -7,7 +7,8 @@ SCRATCH = {
     "PRI": ("sbuf", [128, 128], I32), "PB0": ("sbuf", [128, 128], BF), "PB1": ("sbuf", [128, 128], BF),
     "TI": ("sbuf", [128, 16, 32], I32), "TX": ("sbuf", [128, 16, 32], F16), "TT": ("sbuf", [128, 16, 32], F16),
     "X": ("sbuf", [128, 2048], BF), "VALB": ("sbuf", [128, 4096], BF), "PW": ("sbuf", [128, 2048], I32),
-    "IM": ("sbuf", [128, 160], I32), "I8": ("sbuf", [128, 128], I32), "KP": ("sbuf", [128, 1], I32), "T8I": ("sbuf", [128, 64], I32),
+    "IM": ("sbuf", [128, 160], I32), "I8": ("sbuf", [128, 128], I32), "I16": ("sbuf", [128, 128], I32),
+    "KP": ("sbuf", [128, 1], I32), "T8I": ("sbuf", [128, 64], I32),
     "CI": ("sbuf", [128, 8], I32), "CF": ("sbuf", [128, 8], F32), "CG": ("sbuf", [128, 8], F32),
     "BO": ("sbuf", [128, 128], BF), "TM": ("sbuf", [128, 128], BF), "ID": ("sbuf", [128, 128], BF), "IDH": ("sbuf", [128, 128], F16),
     "PM": ("sbuf", [128, 512], F16), "Z2": ("sbuf", [128, 144], F16), "Z2T": ("sbuf", [128, 144], F16), "ZN": ("sbuf", [128, 144], F16),
@@ -18,8 +19,8 @@ SCRATCH = {
     "KS0": ("sbuf", [128, 64], U16), "KS1": ("sbuf", [128, 64], U16), "KL0": ("sbuf", [128, 64], U16), "KL1": ("sbuf", [128, 64], U16),
     "VS0": ("sbuf", [128, 1024], BF), "VS1": ("sbuf", [128, 1024], BF), "VR0": ("sbuf", [128, 1024], BF), "VR1": ("sbuf", [128, 1024], BF),
     "PROD": ("sbuf", [128, 1024], F16), "EM": ("sbuf", [128, 512], F32), "EA": ("sbuf", [128, 256], F32), "EB": ("sbuf", [128, 128], F32),
-    "AB": ("sbuf", [128, 128], F32), "NI": ("sbuf", [128, 128], I32), "NM": ("sbuf", [128, 128], F32), "PK": ("sbuf", [128, 128], F32),
-    "SMP": ("sbuf", [128, 128], F32), "YO": ("sbuf", [128, 128], F32), "WS": ("sbuf", [128, 7], BF), "WF": ("sbuf", [128, 7], F32),
+    "AB": ("sbuf", [128, 128], F32), "NI": ("sbuf", [128, 128], I32), "PK": ("sbuf", [128, 128], F32), "KEEP": ("sbuf", [128, 128], F32),
+    "YO": ("sbuf", [128, 128], F32), "WS": ("sbuf", [128, 7], BF), "WF": ("sbuf", [128, 7], F32),
     "WR": ("sbuf", [128, 32], BF), "WG": ("sbuf", [128, 32], F32), "DG": ("sbuf", [128, 28 * 128], BF),
     "QA": ("psum", [128, 512], F32), "QB": ("psum", [128, 512], F32), "QT": ("psum", [128, 512], F32), "QE": ("psum", [128, 512], F32),
 }
@@ -30,10 +31,10 @@ for _n in LISTS[1:5]:
     SCRATCH["R" + _n] = ("sbuf", [128, 1024], F16)
 for _q in range(4):
     SCRATCH["H%d" % _q] = ("psum", [128, 512], F32)
-SEMAPHORES = (["dpri", "dtab", "dw", "dx", "dval", "dpw", "dy", "gi", "gz", "vc", "vc2", "vc3", "vi8", "ves", "vbo", "vtm", "vtm2", "vpb", "vperm",
-               "vcv", "vtr", "vsel", "vone", "vid", "vscan", "vS", "vr", "vnf", "vcode", "vmsk", "vmk", "vmn", "vmp", "vpk", "eK", "gV", "vrw4", "vdg",
-               "vpr", "vem", "va1", "va2", "vni", "vnm", "vP", "ptab", "pA", "pB", "pK", "ph", "pE", "swf", "sdg", "swg", "sdg2", "sab",
-               "wl", "wr", "kl", "kr0", "kr1", "vl"]
+SEMAPHORES = (["dpri", "dtab", "dw", "dx", "dval", "dpw", "dy", "gi", "gz", "vz", "vc", "vc2", "vc3", "vi8", "ves", "vbo", "vtm", "vtm2", "vpb", "vperm",
+               "vcv", "vtr", "vsel", "vz4", "vone", "vid", "vscan", "vS", "vr", "vnf", "vcode", "vmsk", "vmk", "vmn", "vmp", "vpk", "vkeep", "eK", "eO", "gV",
+               "vrw4", "vdg", "vpr", "vem", "va1", "va2", "vni", "vP", "ptab", "pA", "pB", "pK", "ph0", "ph1", "ph2", "ph3", "pE", "swf", "sdg", "swg",
+               "sdg2", "sab", "wl", "wr", "kl", "kr0", "kr1", "vl"]
               + ["e" + n for n in LISTS] + ["p" + n for n in LISTS] + ["s" + n for n in LISTS] + ["g" + n for n in LISTS[1:5]]
               + ["vr%d_%d" % (a, q) for a in range(2) for q in range(4)])
 
@@ -59,6 +60,7 @@ def rank_program(g, core, T, topo):
                 got[(q, n)] = tot[n]
 
     peers = [c for c in T.cores if c != core]
+    others = [T.rank_of(c) for c in peers]
 
     def engines_of(src):
         ps = [c for c in T.cores if c != src]
@@ -89,18 +91,19 @@ def rank_program(g, core, T, topo):
         tot[local] = tot.get(local, 0) + sum(len(eng[c]) for c in peers)
 
     done(g.sync.dma_start(T.PRI[:], T.pri[:]), "dpri", 16)
-    done(S.dma_start(T.TI[:, 0:4, :], T.key[:]), "dtab", 16)
-    done(g.sync.dma_start(T.TI[:, 4:8, :], T.nxt[:]), "dtab", 16)
-    done(S.dma_start(T.TI[:, 8:12, :], T.prv[:]), "dtab", 16)
-    done(g.sync.dma_start(T.TI[:, 12:16, :], T.rw[:]), "dtab", 16)
     done(S.dma_start(T.WS[:], T.w[:]), "dw", 16)
+    done(g.sync.dma_start(T.TI[:, 0:4, :], T.key[:]), "dtab", 16)
+    done(S.dma_start(T.TI[:, 4:8, :], T.nxt[:]), "dtab", 16)
+    done(g.sync.dma_start(T.TI[:, 8:12, :], T.prv[:]), "dtab", 16)
+    done(S.dma_start(T.TI[:, 12:16, :], T.rw[:]), "dtab", 16)
     done(S.dma_start(T.X[:], T.x[:]), "dx", 16)
 
     done(g.iota(T.IM[:], [[1, 160]], -16, 0), "gi")
     done(g.iota(T.KP[:], [[0, 1]], 0, 1), "gi")
     done(g.iota(T.T8I[:], [[0, 4], [128, 16]], 0, 0), "gi")
-    done(g.iota(T.PW[:], [[0, 2048]], 0, 0), "gz")
-    need("y", "gz")
+    done(g.iota(T.PW[:, 1024:2048], [[0, 1024]], 0, 0), "gz")
+    done(V.memset(T.PW[:, 0:1024], 0), "vz")
+    need("y", "gz", "vz")
     done(g.sync.dma_start(T.PW[0:128:16, :], T.nxt[:]), "dpw", 16)
     done(g.sync.dma_start(T.PW[1:128:16, :], T.prv[:]), "dpw", 16)
     done(g.sync.dma_start(T.PW[2:128:16, :], T.rw[:]), "dpw", 16)
@@ -109,6 +112,7 @@ def rank_program(g, core, T, topo):
     send(lambda r: T.WS[:], lambda r: T.WR[:, 8 * rank:8 * rank + 7], lambda r: T.sem.wr, "wl")
     tot["wr"] = sum(inc.values())
 
+    done(V.memset(T.ONE[:], 1.0), "vone")
     need("v", "gi")
     kp = T.KP[:]
     m = T.IM[:, 16:144]
@@ -116,69 +120,34 @@ def rank_program(g, core, T, topo):
     def bits(j, sh, msk):
         done(V.tensor_scalar(T.CI[:, j:j + 1], kp, sh, msk, A.logical_shift_right, A.bitwise_and), "vc")
 
-    bits(0, 3, 30)
-    bits(1, 0, 15)
-    bits(2, 0, 7)
-    bits(3, 0, 112)
-    bits(4, 3, 1)
-    bits(5, 4, 1)
-    bits(6, 0, 127)
-    bits(7, 0, 127)
-    done(V.tensor_scalar(T.I8[:], m, 3, None, A.logical_shift_right), "vi8")
-    need("v", "vc")
-    done(V.tensor_copy(T.CF[:], T.CI[:]), "vc2")
-    need("v", "vc2", "vi8")
     cf = lambda j: T.CF[:, j:j + 1]
     cg = lambda j: T.CG[:, j:j + 1]
-    done(V.tensor_scalar(cg(0), cf(0), 1.0, None, A.add), "vc3")
-    done(V.tensor_tensor(cg(1), cf(3), cf(4), A.add), "vc3")
-    done(V.tensor_scalar(cg(2), cf(1), 0.0, None, A.is_equal), "vc3")
-    done(V.tensor_scalar(cg(3), cf(1), 1.0, None, A.is_equal), "vc3")
-    done(V.tensor_scalar(cg(4), cf(1), 2.0, None, A.is_equal), "vc3")
-    done(V.tensor_scalar(cg(5), cf(5), 0.0, None, A.is_equal), "vc3")
-    done(V.tensor_scalar(cg(6), cf(6), 1.0, None, A.subtract), "vc3")
-    done(V.tensor_scalar(cg(7), cf(1), 8.0, None, A.mult), "vc3")
-    done(V.tensor_scalar(T.TM[:], m, cf(6), -1.0, A.is_lt, A.mult), "vtm")
-    done(V.tensor_scalar(T.ES[:, 0:128], T.I8[:], cf(0), None, A.is_equal), "ves")
-    need("v", "vc3")
-    done(V.tensor_scalar(T.ES[:, 128:256], T.I8[:], cg(0), None, A.is_equal), "ves")
-    need("v", "ves", "vtm")
-    done(V.tensor_tensor(T.BO[:], T.ES[:, 0:128], T.ES[:, 128:256], A.add), "vbo")
-    need("v", "vbo")
+    bits(0, 4, 7)
+    bits(1, 4, 1)
+    bits(2, 0, 127)
+    bits(3, 0, 15)
+    bits(4, 0, 7)
+    bits(5, 0, 112)
+    bits(6, 3, 1)
+    done(V.tensor_scalar(T.I16[:], m, 4, None, A.logical_shift_right), "vi8")
+    need("v", "vc")
+    done(V.tensor_copy(T.CF[:, 0:7], T.CI[:, 0:7]), "vc2")
+    need("v", "vc2", "vi8")
+    done(V.tensor_scalar(T.BO[:], T.I16[:], cf(0), None, A.is_equal), "vbo")
+    done(V.tensor_scalar(T.TM[:], m, cf(2), -1.0, A.is_lt, A.mult), "vtm")
+    done(V.tensor_tensor(cg(1), cf(5), cf(6), A.add), "vc3")
+    done(V.tensor_scalar(cg(5), cf(1), 0.0, None, A.is_equal), "vc3")
+    done(V.tensor_scalar(cg(7), cf(3), 8.0, None, A.mult), "vc3")
+    need("v", "vbo", "vtm")
     done(V.tensor_tensor(T.TM[:], T.TM[:], T.BO[:], A.mult), "vtm2")
-    done(V.memset(T.ONE[:], 1.0), "vone")
     need("v", "dpri")
     done(V.tensor_copy(T.PB0[:], T.PRI[:]), "vpb")
-    for n, (lo, col, msk) in enumerate([(16, cf(6), cg(5)), (32, cf(6), cf(5)), (0, cf(6), cg(5)), (16, cf(6), cf(5))]):
-        done(V.tensor_scalar(T.PM[:, 128 * n:128 * n + 128], T.IM[:, lo:lo + 128], col, msk, A.is_equal, A.mult), "vperm")
-    need("v", "dtab")
-    done(V.tensor_scalar(T.TX[:, 0:4, :], T.TI[:, 0:4, :], 2048.0, None, A.subtract), "vcv")
-    done(V.tensor_copy(T.TX[:, 4:16, :], T.TI[:, 4:16, :]), "vcv")
-    need("v", "vcv")
-    done(V.transpose(T.TT[:], T.TX[:]), "vtr")
-
-    def sums(a):
-        pb = T.PB0 if a == 0 else T.PB1
-        need("t", "vbo", "vpb" if a == 0 else "vP")
-        done(P.matmul(T.QA[:, 0:128], T.BO[:], pb[:], True, True), "pA")
-        need("t", "vtm2")
-        done(P.matmul(T.QB[:, 0:128], T.TM[:], pb[:], True, True), "pB")
-
-    sums(0)
-    need("t", "vperm", "vtr")
-    for b1 in range(8):
-        bt = b1 % 2
-        for ga in range(2):
-            n = 2 * ga + bt
-            ins = P.matmul(T.QT[:, b1:512:8], T.PM[:, 128 * n:128 * n + 128], T.TT[:, b1 // 2:16:4, 16 * ga:16 * ga + 16], ga == 0, ga == 1)
-        if b1 == 7:
-            done(ins, "ptab")
-
-    done(V.tensor_scalar(T.Z2T[:], T.IM[:, 0:144], cg(1), cf(2), A.is_equal, A.mult), "vsel")
-    done(V.tensor_scalar(T.Z2[:], T.IM[:, 0:144], cg(1), None, A.is_equal), "vsel")
-    done(V.tensor_scalar(T.IDH[:], m, cf(6), None, A.is_equal), "vsel")
-    done(V.tensor_scalar(T.T8H[:], T.T8I[:], cg(7), None, A.add), "vsel")
-    done(V.tensor_scalar(T.ID[:], m, cf(6), None, A.is_equal), "vid")
+    need("v", "vc3")
+    done(V.tensor_scalar(T.Z2T[:], T.IM[:, 0:144], cg(1), cf(4), A.is_equal, A.mult), "vz4")
+    done(V.tensor_scalar(T.Z2[:], T.IM[:, 0:144], cg(1), None, A.is_equal), "vz4")
+    done(V.tensor_scalar(T.IDH[:], m, cf(2), None, A.is_equal), "vz4")
+    done(V.tensor_scalar(T.T8H[:], T.T8I[:], cg(7), None, A.add), "vz4")
+    done(V.tensor_scalar(T.ID[:], m, cf(2), None, A.is_equal), "vid")
 
     need("s", "dw", "vid")
     done(S.activation(T.WF[:], T.WS[:], COPY), "swf")
@@ -187,13 +156,50 @@ def rank_program(g, core, T, topo):
         o = (7 * rank + d) * 128
         done(S.activation(T.DG[:, o:o + 128], T.ID[:], COPY, scale=T.WF[:, d:d + 1]), "sdg")
 
-    def late_selectors():
-        done(V.tensor_scalar(T.ZN[:], T.IM[:, 0:144], cf(6), cg(2), A.is_equal, A.mult), "vsel")
-        done(V.tensor_scalar(T.ZP[:], T.IM[:, 0:144], cg(6), cg(3), A.is_equal, A.mult), "vsel")
-        done(V.tensor_scalar(T.ER[:, 0:128], T.I8[:], cf(0), cg(4), A.is_equal, A.mult), "vsel")
-        done(V.tensor_scalar(T.ER[:, 128:256], T.I8[:], cg(0), cg(4), A.is_equal, A.mult), "vsel")
+    def sums(a):
+        pb = T.PB0 if a == 0 else T.PB1
+        need("t", "vbo", "vpb" if a == 0 else "vP")
+        done(P.matmul(T.QA[:, 0:128], T.BO[:], pb[:], True, True), "pA")
+        need("t", "vtm2")
+        done(P.matmul(T.QB[:, 0:128], T.TM[:], pb[:], True, True), "pB")
 
-    others = [T.rank_of(c) for c in peers]
+    def permutations():
+        for n, (lo, msk) in enumerate([(16, cg(5)), (32, cf(1)), (0, cg(5)), (16, cf(1))]):
+            done(V.tensor_scalar(T.PM[:, 128 * n:128 * n + 128], T.IM[:, lo:lo + 128], cf(2), msk, A.is_equal, A.mult), "vperm")
+
+    def tables_out():
+        need("t", "vperm", "vtr")
+        for b1 in range(8):
+            bt = b1 % 2
+            for ga in range(2):
+                n = 2 * ga + bt
+                ins = P.matmul(T.QT[:, b1:512:8], T.PM[:, 128 * n:128 * n + 128], T.TT[:, b1 // 2:16:4, 16 * ga:16 * ga + 16], ga == 0, ga == 1)
+            if b1 == 7:
+                done(ins, "ptab")
+
+    def wrap_selectors():
+        done(V.tensor_scalar(cg(2), cf(3), 0.0, None, A.is_equal), "vc3")
+        done(V.tensor_scalar(cg(3), cf(3), 1.0, None, A.is_equal), "vc3")
+        done(V.tensor_scalar(cg(6), cf(2), 1.0, None, A.subtract), "vc3")
+        need("v", "vc3")
+        done(V.tensor_scalar(T.ZN[:], T.IM[:, 0:144], cf(2), cg(2), A.is_equal, A.mult), "vsel")
+        done(V.tensor_scalar(T.ZP[:], T.IM[:, 0:144], cg(6), cg(3), A.is_equal, A.mult), "vsel")
+
+    def frame_selectors():
+        done(V.tensor_scalar(cg(4), cf(3), 2.0, None, A.is_equal), "vc3")
+        done(V.tensor_scalar(cg(0), cf(0), 2.0, 1.0, A.mult, A.add), "vc3")
+        done(V.tensor_scalar(cg(7), cf(0), 2.0, None, A.mult), "vc3")
+        done(V.tensor_scalar(T.I8[:], m, 3, None, A.logical_shift_right), "vc3")
+        for q in range(4):
+            done(V.tensor_copy(T.RW4[:, 128 * q:128 * q + 128], T.QT[:, RWC:RWC + 128]), "vrw4")
+        need("v", "vc3")
+        for ih in range(2):
+            col = cg(0) if ih else cg(7)
+            done(V.tensor_scalar(T.ER[:, 128 * ih:128 * ih + 128], T.I8[:], col, cg(4), A.is_equal, A.mult), "vrw4")
+        for ih in range(2):
+            col = cg(0) if ih else cg(7)
+            done(V.tensor_scalar(T.ES[:, 128 * ih:128 * ih + 128], T.I8[:], col, None, A.is_equal), "ves")
+
     KEYC, NXTC, PRVC, RWC = 0, 128, 256, 384
     STEP = {"L0": 3, "L1": 4, "L2": 5, "L3": 6, "M1": 2, "M2": 1, "M3": 0}
 
@@ -211,7 +217,7 @@ def rank_program(g, core, T, topo):
         need("v", "p" + lst)
         done(V.tensor_copy(T[lst][:], T[bank][:, 0:64]), "e" + lst)
 
-    def mul(a, out, col, sem):
+    def mul(out, col, sem):
         for q in range(4):
             done(V.tensor_tensor(T[out][:, 128 * q:128 * q + 128], T.M4[:, 128 * q:128 * q + 128], T.QT[:, col:col + 128], A.mult), sem)
 
@@ -225,11 +231,11 @@ def rank_program(g, core, T, topo):
 
     def hsum(lst, k):
         need("t", "s" + lst)
-        for q in range(4):
+        for q in [rank] + others:
             o = (7 * q + STEP[lst]) * 128
             ins = P.matmul(T["H%d" % q][:, 0:256], T.DG[:, o:o + 128], T["X" + lst][:, 256 * q:256 * q + 256], k == 0, k == 6)
             if k == 6:
-                done(ins, "ph")
+                done(ins, "ph%d" % q)
 
     def esum(sel, rows, last):
         for ih in range(2):
@@ -237,49 +243,64 @@ def rank_program(g, core, T, topo):
         if last:
             done(ins, "pE")
 
+    def rewards():
+        need("t", "vrw4")
+        P.matmul(T.QE[:], T.IDH[:], T.RW4[:], True, False)
+        esum("ER", "RL1", False)
+        esum("ER", "RL2", False)
+
     for a in range(2):
         pb = T.PB0 if a == 0 else T.PB1
         KS, KL, VS, VR = T["KS%d" % a], T["KL%d" % a], T["VS%d" % a], T["VR%d" % a]
-        if a:
-            sums(a)
+        sums(a)
         need("v", "pA", "vone")
         done(V.tensor_tensor_scan(T.CS[:], T.ONE[:], T.QA[:, 0:128], 0.0, A.mult, A.add), "vscan")
+        if a == 0:
+            permutations()
         need("v", "pB", "vscan")
         done(V.tensor_tensor(T.SI[:], T.CS[:], T.QB[:, 0:128], A.add), "vS")
         need("v", "vS")
         done(V.tensor_scalar(T.RI[:], T.SI[:], 127, None, A.bitwise_and), "vr")
         done(V.tensor_scalar(T.K2[:], T.SI[:], 6, 6, A.arith_shift_right, A.bitwise_and), "vr")
+        if a == 0:
+            need("v", "dtab")
+            done(V.tensor_scalar(T.TX[:, 0:4, :], T.TI[:, 0:4, :], 2048.0, None, A.subtract), "vcv")
+            done(V.tensor_copy(T.TX[:, 4:16, :], T.TI[:, 4:16, :]), "vcv")
         need("v", "vr")
         done(V.tensor_tensor(T.NF[:], T.RI[:], pb[:], A.is_ge), "vnf")
+        if a == 0:
+            need("v", "vcv")
+            done(V.transpose(T.TT[:], T.TX[:]), "vtr")
+            tables_out()
         need("v", "vnf")
         done(V.tensor_tensor(T.CODE[:], T.K2[:], T.NF[:], A.add), "vcode")
         need("v", "vcode")
         for q in range(4):
             done(V.tensor_scalar(T.M4[:, 128 * q:128 * q + 128], T.CODE[:], float(2 * ((q + 1) % 4)), None, A.is_equal), "vmsk")
-        need("t", "vmsk", "vsel", "vscan")
+        need("t", "vmsk", "vz4", "vscan")
         P.matmul(T.QA[:, 0:64], T.IDH[:], T.T8H[:], True, False)
         blocksum("pL0", "QA", "Z2T", "M4", False)
         need("v", "vmsk", "ptab")
-        mul(a, "MK", KEYC, "vmk")
+        mul("MK", KEYC, "vmk")
         need("t", "vmk", "vS")
         blocksum("pK", "QB", "Z2", "MK")
         evac("L0", "QA")
         pick_x("L0")
-        mul(a, "MN", NXTC, "vmn")
+        mul("MN", NXTC, "vmn")
         need("t", "vmn", "eL0")
         blocksum("pL1", "QA", "Z2", "MN")
         need("v", "pK")
         done(V.tensor_scalar(KS[:], T.QB[:, 0:64], 2048.0, None, A.add), "eK")
-        done(V.tensor_scalar(KL[:, 16 * rank:16 * rank + 16], T.QB[:, 16 * rank:16 * rank + 16], 2048.0, None, A.add), "eK")
+        done(V.tensor_scalar(KL[:, 16 * rank:16 * rank + 16], T.QB[:, 16 * rank:16 * rank + 16], 2048.0, None, A.add), "eO")
         kr = "kr%d" % a
         need("g", "eK")
         send(lambda r: KS[:, 16 * r:16 * r + 16], lambda r: KL[:, 16 * rank:16 * rank + 16], lambda r: T.sem[kr], "kl")
         tot[kr] = sum(inc.values())
-        mul(a, "MP", PRVC, "vmp")
-        need("t", "vmp", "eK")
+        mul("MP", PRVC, "vmp")
+        need("t", "vmp", "eK", "eO")
         blocksum("pM1", "QB", "Z2", "MP")
         if a == 0:
-            late_selectors()
+            wrap_selectors()
         evac("L1", "QA")
         pick_p("L1")
         evac("M1", "QB")
@@ -295,58 +316,56 @@ def rank_program(g, core, T, topo):
                 done(S.activation(T.DG[:, (7 * o + d) * 128:(7 * o + d) * 128 + 128], T.ID[:], COPY, scale=T.WG[:, d:d + 1]), "sdg2")
         pick_x("L1")
         pick_x("M1")
+        need("s", "dval", kr, "eO")
+        done(S.activation(VS[:], T.VALB[:].indirect(KL[:]), COPY), "gV")
+        need("g", "gV")
+        send(lambda r: VS[:, 256 * r:256 * r + 256], lambda r: VR[:, 256 * rank:256 * rank + 256], lambda r: T.sem["vr%d_%d" % (a, rank)], "vl")
+        for c in peers:
+            tot["vr%d_%d" % (a, T.rank_of(c))] = inc[c]
         evac("L2", "QA")
         pick_x("L2")
         need("t", "eM1", "gM1")
         wrap("M2", "QB", "ZP", "RM1")
         if a == 0:
-            for q in range(4):
-                done(V.tensor_copy(T.RW4[:, 128 * q:128 * q + 128], T.QT[:, RWC:RWC + 128]), "vrw4")
-            need("v", "wr", "vid")
+            need("v", "wr")
             for o in others[1:]:
                 for d in range(7):
                     done(V.tensor_scalar(T.DG[:, (7 * o + d) * 128:(7 * o + d) * 128 + 128], T.ID[:], T.WR[:, 8 * o + d:8 * o + d + 1], None, A.mult), "vdg")
-        evac("M2", "QB")
-        pick_x("M2")
-        need("v", "dval", kr, "eK")
-        done(V.tensor_copy(VS[:], T.VALB[:].indirect(KL[:])), "gV")
-        need("g", "gV")
-        send(lambda r: VS[:, 256 * r:256 * r + 256], lambda r: VR[:, 256 * rank:256 * rank + 256], lambda r: T.sem["vr%d_%d" % (a, rank)], "vl")
-        for c in peers:
-            tot["vr%d_%d" % (a, T.rank_of(c))] = inc[c]
         pick_p("L2")
+        evac("M2", "QB")
         pick_p("M2")
-        need("t", "vrw4")
-        P.matmul(T.QE[:], T.IDH[:], T.RW4[:], True, False)
-        esum("ER", "RL1", False)
+        pick_x("M2")
         need("t", "sdg", "sdg2", "vdg")
         hsum("L0", 0)
         hsum("L1", 1)
-        hsum("M1", 2)
         need("t", "eL2", "gL2")
         wrap("L3", "QA", "ZN", "RL2")
+        hsum("M1", 2)
         evac("L3", "QA")
         pick_x("L3")
-        hsum("L2", 3)
         need("t", "eM2", "gM2")
         wrap("M3", "QB", "ZP", "RM2")
         evac("M3", "QB")
-        pick_x("M3")
+        need("v", "dx", "eM3")
+        done(V.tensor_copy(T.XM3[:], T.X[:].indirect(T.M3[:])), "sM3")
         done(V.tensor_tensor(T.PK[:], T.NF[:], pb[:], A.mult), "vpk")
-        done(V.tensor_scalar(T.SMP[:], T.NF[:], -1.0, 1.0, A.mult, A.add), "vpk")
-        esum("ER", "RL2", False)
+        if a == 0:
+            frame_selectors()
+        else:
+            rewards()
+        need("v", "vpk")
+        done(V.tensor_scalar(T.KEEP[:], T.PK[:], 1.0, None, A.max), "vkeep")
+        hsum("L2", 3)
         hsum("M2", 4)
-        hsum("L3", 5)
-        hsum("M3", 6)
-        need("v", "ph")
+        hsum("M3", 5)
+        hsum("L3", 6)
+        if a == 0:
+            rewards()
         for q in [rank] + others:
-            if q != rank:
-                need("v", "vr%d_%d" % (a, q))
+            need("v", "ph%d" % q, "gV" if q == rank else "vr%d_%d" % (a, q))
             src = VS if q == rank else VR
-            if q == rank:
-                need("v", "gV")
             done(V.tensor_tensor(T.PROD[:, 256 * q:256 * q + 256], src[:, 256 * q:256 * q + 256], T["H%d" % q][:, 0:256], A.mult), "vpr")
-        need("t", "vpr")
+        need("t", "vpr", "ves")
         esum("ES", "PROD", True)
         need("v", "pE")
         done(V.tensor_tensor(T.EM[:], T.M4[:], T.QE[:], A.mult), "vem")
@@ -356,12 +375,10 @@ def rank_program(g, core, T, topo):
         done(V.tensor_tensor(T.EB[:], T.EA[:, 0:128], T.EA[:, 128:256], A.add), "va2")
         need("s", "va2")
         done(S.activation(T.AB[:], T.EB[:], ABS, scale=0.0625), "sab")
-        need("v", "sab", "vpk")
+        need("v", "sab", "vkeep")
         done(V.tensor_scalar(T.NI[:], T.AB[:], 0.46875, 63.0, A.subtract, A.min), "vni")
         need("v", "vni")
-        done(V.tensor_tensor(T.NM[:], T.NI[:], T.SMP[:], A.max), "vnm")
-        need("v", "vnm")
-        done(V.tensor_tensor((T.YO if a else T.PB1)[:], T.NM[:], T.PK[:], A.add), "vP")
+        done(V.tensor_tensor((T.YO if a else T.PB1)[:], T.NI[:], T.KEEP[:], A.max), "vP")
     need("y", "vP")
     done(g.sync.dma_start(T.y[:], T.YO[:]), "dy", 16)
     need("y", "dy")

@@ -7,22 +7,23 @@ SCRATCH = {
     "PRI": ("sbuf", [128, 128], I32), "PB0": ("sbuf", [128, 128], BF), "PB1": ("sbuf", [128, 128], BF),
     "TI": ("sbuf", [128, 16, 32], I32), "TX": ("sbuf", [128, 16, 32], F16), "TT": ("sbuf", [128, 16, 32], F16),
     "X": ("sbuf", [128, 2048], BF), "VALB": ("sbuf", [128, 4096], BF), "PW": ("sbuf", [128, 2048], I32),
-    "IM": ("sbuf", [128, 160], I32), "I8": ("sbuf", [128, 128], I32), "I16": ("sbuf", [128, 128], I32),
-    "KP": ("sbuf", [128, 1], I32), "T8I": ("sbuf", [128, 64], I32),
+    "IM": ("sbuf", [128, 160], I32), "I16": ("sbuf", [128, 128], I32), "KP": ("sbuf", [128, 1], I32), "T8I": ("sbuf", [128, 64], I32),
     "CI": ("sbuf", [128, 8], I32), "CF": ("sbuf", [128, 8], F32), "CG": ("sbuf", [128, 8], F32),
-    "BO": ("sbuf", [128, 128], BF), "TM": ("sbuf", [128, 128], BF), "ID": ("sbuf", [128, 128], BF), "IDH": ("sbuf", [128, 128], F16),
-    "PM": ("sbuf", [128, 512], F16), "Z2": ("sbuf", [128, 144], F16), "Z2T": ("sbuf", [128, 144], F16), "ZN": ("sbuf", [128, 144], F16),
-    "ZP": ("sbuf", [128, 144], F16), "ES": ("sbuf", [128, 256], F16), "ER": ("sbuf", [128, 256], F16), "T8H": ("sbuf", [128, 64], F16),
+    "BO": ("sbuf", [128, 128], BF), "TM": ("sbuf", [128, 128], BF), "IDW": ("sbuf", [128, 160], BF), "ONB": ("sbuf", [128, 144], BF),
+    "C16": ("sbuf", [128, 128], BF), "PM": ("sbuf", [128, 512], BF), "Z2": ("sbuf", [128, 144], F16), "Z2T": ("sbuf", [128, 144], F16),
+    "ZN": ("sbuf", [128, 144], BF), "ZP": ("sbuf", [128, 144], BF), "ES": ("sbuf", [128, 256], BF), "ER": ("sbuf", [128, 256], BF),
+    "T8H": ("sbuf", [128, 64], F16), "PV": ("sbuf", [128, 128], U16),
     "ONE": ("sbuf", [128, 128], F32), "CS": ("sbuf", [128, 128], F32), "SI": ("sbuf", [128, 128], I32), "RI": ("sbuf", [128, 128], I32),
     "K2": ("sbuf", [128, 128], I32), "NF": ("sbuf", [128, 128], F32), "CODE": ("sbuf", [128, 128], F16), "M4": ("sbuf", [128, 512], F16),
     "MK": ("sbuf", [128, 512], F16), "MN": ("sbuf", [128, 512], F16), "MP": ("sbuf", [128, 512], F16), "RW4": ("sbuf", [128, 512], F16),
     "KS0": ("sbuf", [128, 64], U16), "KS1": ("sbuf", [128, 64], U16), "KL0": ("sbuf", [128, 64], U16), "KL1": ("sbuf", [128, 64], U16),
     "VS0": ("sbuf", [128, 1024], BF), "VS1": ("sbuf", [128, 1024], BF), "VR0": ("sbuf", [128, 1024], BF), "VR1": ("sbuf", [128, 1024], BF),
-    "PROD": ("sbuf", [128, 1024], F16), "EM": ("sbuf", [128, 512], F32), "EA": ("sbuf", [128, 256], F32), "EB": ("sbuf", [128, 128], F32),
-    "AB": ("sbuf", [128, 128], F32), "NI": ("sbuf", [128, 128], I32), "PK": ("sbuf", [128, 128], F32), "KEEP": ("sbuf", [128, 128], F32),
-    "YO": ("sbuf", [128, 128], F32), "WS": ("sbuf", [128, 7], BF), "WF": ("sbuf", [128, 7], F32),
+    "PROD": ("sbuf", [128, 1024], F16), "EM": ("sbuf", [128, 256], F32), "EA": ("sbuf", [128, 128], F32), "EB": ("sbuf", [128, 128], F32),
+    "EC": ("sbuf", [128, 128], F32), "AB": ("sbuf", [128, 128], F32), "NI": ("sbuf", [128, 128], I32), "PK": ("sbuf", [128, 128], F32),
+    "KEEP": ("sbuf", [128, 128], F32), "YO": ("sbuf", [128, 128], F32), "WS": ("sbuf", [128, 7], BF), "WF": ("sbuf", [128, 7], F32),
     "WR": ("sbuf", [128, 32], BF), "WG": ("sbuf", [128, 32], F32), "DG": ("sbuf", [128, 28 * 128], BF),
     "QA": ("psum", [128, 512], F32), "QB": ("psum", [128, 512], F32), "QT": ("psum", [128, 512], F32), "QE": ("psum", [128, 512], F32),
+    "XT1": ("sbuf", [128, 2048], BF), "XT2": ("sbuf", [128, 2048], BF),
 }
 for _n in LISTS:
     SCRATCH[_n] = ("sbuf", [128, 64], U16)
@@ -31,10 +32,11 @@ for _n in LISTS[1:5]:
     SCRATCH["R" + _n] = ("sbuf", [128, 1024], F16)
 for _q in range(4):
     SCRATCH["H%d" % _q] = ("psum", [128, 512], F32)
-SEMAPHORES = (["dpri", "dtab", "dw", "dx", "dval", "dpw", "dy", "gi", "gz", "vz", "vc", "vc2", "vc3", "vi8", "ves", "vbo", "vtm", "vtm2", "vpb", "vperm",
-               "vcv", "vtr", "vsel", "vz4", "vone", "vid", "vscan", "vS", "vr", "vnf", "vcode", "vmsk", "vmk", "vmn", "vmp", "vpk", "vkeep", "eK", "eO", "gV",
-               "vrw4", "vdg", "vpr", "vem", "va1", "va2", "vni", "vP", "ptab", "pA", "pB", "pK", "ph0", "ph1", "ph2", "ph3", "pE", "swf", "sdg", "swg",
-               "sdg2", "sab", "wl", "wr", "kl", "kr0", "kr1", "vl"]
+SEMAPHORES = (["dpri", "dtab", "dw", "dx", "dval", "dpw", "dy", "gi", "gz", "gsel", "ges", "ges2", "vz", "vcon", "vc", "vc2", "vc3", "vi8", "vbo", "vtm",
+               "vtm2", "vpb", "sperm", "vcv", "vtr", "vz4", "vone", "vid", "vpv", "vscan", "vS", "vr", "vnf", "vcode", "vm0", "vm1", "vm2", "vm3",
+               "vmk", "vmn", "vmp", "vpk", "vkeep", "eK", "eO", "gV", "gU", "vrw4", "vdg", "vpr", "vem", "va1", "va2", "va3", "vab", "vni", "vP", "ptab",
+               "pA", "pB", "pK", "ph0", "ph1", "ph2", "ph3", "pE", "swf", "sdg", "swg", "sdg2", "st1", "st2", "wl", "wr", "kl", "vl",
+               "kr0", "kr1", "ko0", "ko1"]
               + ["e" + n for n in LISTS] + ["p" + n for n in LISTS] + ["s" + n for n in LISTS] + ["g" + n for n in LISTS[1:5]]
               + ["vr%d_%d" % (a, q) for a in range(2) for q in range(4)])
 
@@ -59,36 +61,42 @@ def rank_program(g, core, T, topo):
                 Q[q].wait_ge(T.sem[n], tot[n])
                 got[(q, n)] = tot[n]
 
-    peers = [c for c in T.cores if c != core]
-    others = [T.rank_of(c) for c in peers]
+    def off_of(src):
+        return [c for c in T.cores if c not in topo.cores_of(src)]
+
+    def on_of(src):
+        return [c for c in T.cores if c != src and c in topo.cores_of(src)]
 
     def engines_of(src):
-        ps = [c for c in T.cores if c != src]
-        off = [c for c in ps if c not in topo.cores_of(src)]
-        out = {}
+        off, out = off_of(src), {}
         eo = topo.engines(src, off[0])
         n = len(eo) // len(off)
         for k, c in enumerate(off):
             out[c] = eo[k * n:(k + 1) * n]
-        for c in ps:
-            if c not in out:
-                out[c] = [e for e in topo.engines(src, c) if e not in eo]
+        for c in on_of(src):
+            out[c] = [e for e in topo.engines(src, c) if e not in eo]
         return out
 
+    def place(c, at):
+        return (off_of(at) + on_of(at) + [at]).index(c)
+
+    off, on = off_of(core), on_of(core)
+    peers = on + off
+    others = [T.rank_of(c) for c in peers]
+    half = len(off)
     eng = engines_of(core)
     inc = {c: len(engines_of(c)[core]) for c in peers}
 
-    def send(src_of, dst_of, sem_of, local):
+    def send(to, src_of, dst_of, sem_of, local):
         tr = []
-        for c in peers:
+        for c in to:
             rid, pid = topo.addr(c, core)
             m = 0
             for e in eng[c]:
                 m |= 1 << e
-            r = T.rank_of(c)
-            tr.append(RemoteDMATransfer(dst_ids=[DstId(rid=rid, pnc=pid)], dma_engine_mask=m, remote_sem=sem_of(r), src=src_of(r), dst=dst_of(r)))
+            tr.append(RemoteDMATransfer(dst_ids=[DstId(rid=rid, pnc=pid)], dma_engine_mask=m, remote_sem=sem_of(c), src=src_of(c), dst=dst_of(c)))
         g.remote_dma_fused(tr, local_sem=T.sem[local])
-        tot[local] = tot.get(local, 0) + sum(len(eng[c]) for c in peers)
+        tot[local] = tot.get(local, 0) + sum(len(eng[c]) for c in to)
 
     done(g.sync.dma_start(T.PRI[:], T.pri[:]), "dpri", 16)
     done(S.dma_start(T.WS[:], T.w[:]), "dw", 16)
@@ -109,13 +117,14 @@ def rank_program(g, core, T, topo):
     done(g.sync.dma_start(T.PW[2:128:16, :], T.rw[:]), "dpw", 16)
     done(g.sync.dma_start(T.VALB[:], T.val[:]), "dval", 16)
     need("g", "dw")
-    send(lambda r: T.WS[:], lambda r: T.WR[:, 8 * rank:8 * rank + 7], lambda r: T.sem.wr, "wl")
+    send(peers, lambda c: T.WS[:], lambda c: T.WR[:, 8 * rank:8 * rank + 7], lambda c: T.sem.wr, "wl")
     tot["wr"] = sum(inc.values())
 
     done(V.memset(T.ONE[:], 1.0), "vone")
     need("v", "gi")
     kp = T.KP[:]
     m = T.IM[:, 16:144]
+    ident = T.IDW[:, 16:144]
 
     def bits(j, sh, msk):
         done(V.tensor_scalar(T.CI[:, j:j + 1], kp, sh, msk, A.logical_shift_right, A.bitwise_and), "vc")
@@ -135,26 +144,28 @@ def rank_program(g, core, T, topo):
     need("v", "vc2", "vi8")
     done(V.tensor_scalar(T.BO[:], T.I16[:], cf(0), None, A.is_equal), "vbo")
     done(V.tensor_scalar(T.TM[:], m, cf(2), -1.0, A.is_lt, A.mult), "vtm")
-    done(V.tensor_tensor(cg(1), cf(5), cf(6), A.add), "vc3")
     done(V.tensor_scalar(cg(5), cf(1), 0.0, None, A.is_equal), "vc3")
+    done(V.tensor_tensor(cg(1), cf(5), cf(6), A.add), "vc3")
     done(V.tensor_scalar(cg(7), cf(3), 8.0, None, A.mult), "vc3")
     need("v", "vbo", "vtm")
     done(V.tensor_tensor(T.TM[:], T.TM[:], T.BO[:], A.mult), "vtm2")
+    done(V.tensor_scalar(T.IDW[:], T.IM[:], cf(2), None, A.is_equal), "vid")
     need("v", "dpri")
     done(V.tensor_copy(T.PB0[:], T.PRI[:]), "vpb")
     need("v", "vc3")
     done(V.tensor_scalar(T.Z2T[:], T.IM[:, 0:144], cg(1), cf(4), A.is_equal, A.mult), "vz4")
     done(V.tensor_scalar(T.Z2[:], T.IM[:, 0:144], cg(1), None, A.is_equal), "vz4")
-    done(V.tensor_scalar(T.IDH[:], m, cf(2), None, A.is_equal), "vz4")
     done(V.tensor_scalar(T.T8H[:], T.T8I[:], cg(7), None, A.add), "vz4")
-    done(V.tensor_scalar(T.ID[:], m, cf(2), None, A.is_equal), "vid")
 
-    need("s", "dw", "vid")
+    need("s", "vid", "vc3", "vc2")
+    for n, (lo, msk) in enumerate([(16, cg(5)), (32, cf(1)), (0, cg(5)), (16, cf(1))]):
+        done(S.activation(T.PM[:, 128 * n:128 * n + 128], T.IDW[:, lo:lo + 128], COPY, scale=msk), "sperm")
+    need("s", "dw")
     done(S.activation(T.WF[:], T.WS[:], COPY), "swf")
     need("s", "swf")
     for d in range(7):
         o = (7 * rank + d) * 128
-        done(S.activation(T.DG[:, o:o + 128], T.ID[:], COPY, scale=T.WF[:, d:d + 1]), "sdg")
+        done(S.activation(T.DG[:, o:o + 128], ident, COPY, scale=T.WF[:, d:d + 1]), "sdg")
 
     def sums(a):
         pb = T.PB0 if a == 0 else T.PB1
@@ -163,12 +174,8 @@ def rank_program(g, core, T, topo):
         need("t", "vtm2")
         done(P.matmul(T.QB[:, 0:128], T.TM[:], pb[:], True, True), "pB")
 
-    def permutations():
-        for n, (lo, msk) in enumerate([(16, cg(5)), (32, cf(1)), (0, cg(5)), (16, cf(1))]):
-            done(V.tensor_scalar(T.PM[:, 128 * n:128 * n + 128], T.IM[:, lo:lo + 128], cf(2), msk, A.is_equal, A.mult), "vperm")
-
     def tables_out():
-        need("t", "vperm", "vtr")
+        need("t", "sperm", "vtr")
         for b1 in range(8):
             bt = b1 % 2
             for ga in range(2):
@@ -177,31 +184,23 @@ def rank_program(g, core, T, topo):
             if b1 == 7:
                 done(ins, "ptab")
 
-    def wrap_selectors():
-        done(V.tensor_scalar(cg(2), cf(3), 0.0, None, A.is_equal), "vc3")
-        done(V.tensor_scalar(cg(3), cf(3), 1.0, None, A.is_equal), "vc3")
-        done(V.tensor_scalar(cg(6), cf(2), 1.0, None, A.subtract), "vc3")
-        need("v", "vc3")
-        done(V.tensor_scalar(T.ZN[:], T.IM[:, 0:144], cf(2), cg(2), A.is_equal, A.mult), "vsel")
-        done(V.tensor_scalar(T.ZP[:], T.IM[:, 0:144], cg(6), cg(3), A.is_equal, A.mult), "vsel")
-
-    def frame_selectors():
-        done(V.tensor_scalar(cg(4), cf(3), 2.0, None, A.is_equal), "vc3")
-        done(V.tensor_scalar(cg(0), cf(0), 2.0, 1.0, A.mult, A.add), "vc3")
-        done(V.tensor_scalar(cg(7), cf(0), 2.0, None, A.mult), "vc3")
-        done(V.tensor_scalar(T.I8[:], m, 3, None, A.logical_shift_right), "vc3")
-        for q in range(4):
-            done(V.tensor_copy(T.RW4[:, 128 * q:128 * q + 128], T.QT[:, RWC:RWC + 128]), "vrw4")
-        need("v", "vc3")
+    def gpsimd_selectors():
+        need("g", "vcon")
+        done(g.affine_select(T.ZN[:], T.ONB[:], [[-16, 9], [-1000, 16]], A.is_equal, 0.0, 16, 1), "gsel")
+        done(g.affine_select(T.ZP[:], T.ONB[:], [[-16, 9], [-1000, 16]], A.is_equal, 0.0, 15, 1), "gsel")
         for ih in range(2):
-            col = cg(0) if ih else cg(7)
-            done(V.tensor_scalar(T.ER[:, 128 * ih:128 * ih + 128], T.I8[:], col, cg(4), A.is_equal, A.mult), "vrw4")
+            pat, base = [[-16, 8], [1000 if ih else -1000, 2], [0, 8]], -1000 if ih else 0
+            o = slice(128 * ih, 128 * ih + 128)
+            done(g.affine_select(T.ER[:, o], T.C16[:], pat, A.is_equal, 0.0, base - 2, 1), "ges2")
+            done(g.affine_select(T.ES[:, o], T.C16[:], pat, A.is_ge, 0.0, base, 1), "ges")
+        need("g", "ges")
         for ih in range(2):
-            col = cg(0) if ih else cg(7)
-            done(V.tensor_scalar(T.ES[:, 128 * ih:128 * ih + 128], T.I8[:], col, None, A.is_equal), "ves")
+            o = slice(128 * ih, 128 * ih + 128)
+            done(g.affine_select(T.ES[:, o], T.ES[:, o], [[16, 8], [0, 2], [0, 8]], A.is_ge, 0.0, 15, -1), "ges2")
 
     KEYC, NXTC, PRVC, RWC = 0, 128, 256, 384
     STEP = {"L0": 3, "L1": 4, "L2": 5, "L3": 6, "M1": 2, "M2": 1, "M3": 0}
+    MASKS = ["vm0", "vm1", "vm2", "vm3"]
 
     def blocksum(name, bank, sel, rows, first=True):
         for cl in range(8):
@@ -209,6 +208,7 @@ def rank_program(g, core, T, topo):
         done(ins, name)
 
     def wrap(lst, bank, sel, rows):
+        need("t", "gsel")
         for ro in range(16):
             ins = P.matmul(T[bank][:, 0:64], T[sel][:, 16 - ro:144 - ro], T[rows][:, ro:1024:16], ro == 0, ro == 15)
         done(ins, "p" + lst)
@@ -217,13 +217,19 @@ def rank_program(g, core, T, topo):
         need("v", "p" + lst)
         done(V.tensor_copy(T[lst][:], T[bank][:, 0:64]), "e" + lst)
 
-    def mul(out, col, sem):
-        for q in range(4):
+    def mul(out, col, sem, qs=range(4)):
+        for q in qs:
+            need("v", MASKS[q])
             done(V.tensor_tensor(T[out][:, 128 * q:128 * q + 128], T.M4[:, 128 * q:128 * q + 128], T.QT[:, col:col + 128], A.mult), sem)
 
-    def pick_x(lst):
-        need("s", "dx", "e" + lst)
-        done(S.activation(T["X" + lst][:], T.X[:].indirect(T[lst][:]), COPY), "s" + lst)
+    def pick_x(lst, on_q="s", table="X", at=None):
+        at = at or lst
+        need(on_q, "dx", "e" + at)
+        src = T[table][:].indirect(T[at][:])
+        if on_q == "s":
+            done(S.activation(T["X" + lst][:], src, COPY), "s" + lst)
+        else:
+            done(V.tensor_copy(T["X" + lst][:], src), "s" + lst)
 
     def pick_p(lst):
         need("v", "dpw", "e" + lst)
@@ -244,10 +250,26 @@ def rank_program(g, core, T, topo):
             done(ins, "pE")
 
     def rewards():
-        need("t", "vrw4")
-        P.matmul(T.QE[:], T.IDH[:], T.RW4[:], True, False)
+        need("t", "vrw4", "ges2")
+        P.matmul(T.QE[:], ident, T.RW4[:], True, False)
         esum("ER", "RL1", False)
         esum("ER", "RL2", False)
+
+    def serve(a):
+        KL, VS, VR = T["KL%d" % a], T["VS%d" % a], T["VR%d" % a]
+        src = lambda c: VS[:, 256 * place(c, core):256 * place(c, core) + 256]
+        dst = lambda c: VR[:, 256 * rank:256 * rank + 256]
+        sem = lambda c: T.sem["vr%d_%d" % (a, rank)]
+        need("s", "dval", "ko%d" % a)
+        done(S.activation(VS[:, 0:256 * half], T.VALB[:].indirect(KL[:, 0:16 * half]), COPY), "gU")
+        need("s", "kr%d" % a, "eO")
+        done(S.activation(VS[:, 256 * half:1024], T.VALB[:].indirect(KL[:, 16 * half:64]), COPY), "gV")
+        need("g", "gU")
+        send(off, src, dst, sem, "vl")
+        need("g", "gV")
+        send(on, src, dst, sem, "vl")
+        for c in peers:
+            tot["vr%d_%d" % (a, T.rank_of(c))] = inc[c]
 
     for a in range(2):
         pb = T.PB0 if a == 0 else T.PB1
@@ -255,8 +277,6 @@ def rank_program(g, core, T, topo):
         sums(a)
         need("v", "pA", "vone")
         done(V.tensor_tensor_scan(T.CS[:], T.ONE[:], T.QA[:, 0:128], 0.0, A.mult, A.add), "vscan")
-        if a == 0:
-            permutations()
         need("v", "pB", "vscan")
         done(V.tensor_tensor(T.SI[:], T.CS[:], T.QB[:, 0:128], A.add), "vS")
         need("v", "vS")
@@ -276,106 +296,140 @@ def rank_program(g, core, T, topo):
         done(V.tensor_tensor(T.CODE[:], T.K2[:], T.NF[:], A.add), "vcode")
         need("v", "vcode")
         for q in range(4):
-            done(V.tensor_scalar(T.M4[:, 128 * q:128 * q + 128], T.CODE[:], float(2 * ((q + 1) % 4)), None, A.is_equal), "vmsk")
-        need("t", "vmsk", "vz4", "vscan")
-        P.matmul(T.QA[:, 0:64], T.IDH[:], T.T8H[:], True, False)
+            done(V.tensor_scalar(T.M4[:, 128 * q:128 * q + 128], T.CODE[:], float(2 * ((q + 1) % 4)), None, A.is_equal), MASKS[q])
+        need("t", "vz4", "vid", "vscan", *MASKS)
+        P.matmul(T.QA[:, 0:64], ident, T.T8H[:], True, False)
         blocksum("pL0", "QA", "Z2T", "M4", False)
-        need("v", "vmsk", "ptab")
+        need("v", "ptab")
         mul("MK", KEYC, "vmk")
         need("t", "vmk", "vS")
         blocksum("pK", "QB", "Z2", "MK")
         evac("L0", "QA")
         pick_x("L0")
-        mul("MN", NXTC, "vmn")
-        need("t", "vmn", "eL0")
-        blocksum("pL1", "QA", "Z2", "MN")
+        mul("MN", NXTC, "vmn", (0, 1))
         need("v", "pK")
         done(V.tensor_scalar(KS[:], T.QB[:, 0:64], 2048.0, None, A.add), "eK")
-        done(V.tensor_scalar(KL[:, 16 * rank:16 * rank + 16], T.QB[:, 16 * rank:16 * rank + 16], 2048.0, None, A.add), "eO")
-        kr = "kr%d" % a
         need("g", "eK")
-        send(lambda r: KS[:, 16 * r:16 * r + 16], lambda r: KL[:, 16 * rank:16 * rank + 16], lambda r: T.sem[kr], "kl")
-        tot[kr] = sum(inc.values())
+        send(peers, lambda c: KS[:, 16 * T.rank_of(c):16 * T.rank_of(c) + 16], lambda c: KL[:, 16 * place(core, c):16 * place(core, c) + 16],
+             lambda c: T.sem[("ko%d" if c in off else "kr%d") % a], "kl")
+        tot["ko%d" % a] = sum(inc[c] for c in off)
+        tot["kr%d" % a] = sum(inc[c] for c in on)
+        mul("MN", NXTC, "vmn", (2, 3))
+        need("t", "vmn", "eL0")
+        blocksum("pL1", "QA", "Z2", "MN")
+        mine = 16 * place(core, core)
+        done(V.tensor_scalar(KL[:, mine:mine + 16], T.QB[:, 16 * rank:16 * rank + 16], 2048.0, None, A.add), "eO")
+        if a == 0:
+            done(V.memset(T.ONB[:], 1.0), "vcon")
+            done(V.memset(T.C16[:], 0.0625), "vcon")
+            gpsimd_selectors()
         mul("MP", PRVC, "vmp")
         need("t", "vmp", "eK", "eO")
         blocksum("pM1", "QB", "Z2", "MP")
-        if a == 0:
-            wrap_selectors()
         evac("L1", "QA")
         pick_p("L1")
-        evac("M1", "QB")
-        pick_p("M1")
-        need("t", "vsel", "eL1", "gL1")
-        wrap("L2", "QA", "ZN", "RL1")
         if a == 0:
+            evac("M1", "QB")
+            pick_p("M1")
+            need("t", "eL1", "gL1")
+            wrap("L2", "QA", "ZN", "RL1")
             need("s", "wr")
             o = others[0]
             done(S.activation(T.WG[:, 0:7], T.WR[:, 8 * o:8 * o + 7], COPY), "swg")
             need("s", "swg")
             for d in range(7):
-                done(S.activation(T.DG[:, (7 * o + d) * 128:(7 * o + d) * 128 + 128], T.ID[:], COPY, scale=T.WG[:, d:d + 1]), "sdg2")
-        pick_x("L1")
-        pick_x("M1")
-        need("s", "dval", kr, "eO")
-        done(S.activation(VS[:], T.VALB[:].indirect(KL[:]), COPY), "gV")
-        need("g", "gV")
-        send(lambda r: VS[:, 256 * r:256 * r + 256], lambda r: VR[:, 256 * rank:256 * rank + 256], lambda r: T.sem["vr%d_%d" % (a, rank)], "vl")
-        for c in peers:
-            tot["vr%d_%d" % (a, T.rank_of(c))] = inc[c]
-        evac("L2", "QA")
-        pick_x("L2")
-        need("t", "eM1", "gM1")
-        wrap("M2", "QB", "ZP", "RM1")
-        if a == 0:
+                done(S.activation(T.DG[:, (7 * o + d) * 128:(7 * o + d) * 128 + 128], ident, COPY, scale=T.WG[:, d:d + 1]), "sdg2")
+            pick_x("L1")
+            pick_x("M1")
+            serve(a)
+            evac("L2", "QA")
+            pick_x("L2")
+            need("t", "eM1", "gM1")
+            wrap("M2", "QB", "ZP", "RM1")
             need("v", "wr")
             for o in others[1:]:
                 for d in range(7):
-                    done(V.tensor_scalar(T.DG[:, (7 * o + d) * 128:(7 * o + d) * 128 + 128], T.ID[:], T.WR[:, 8 * o + d:8 * o + d + 1], None, A.mult), "vdg")
-        pick_p("L2")
-        evac("M2", "QB")
-        pick_p("M2")
-        pick_x("M2")
-        need("t", "sdg", "sdg2", "vdg")
-        hsum("L0", 0)
-        hsum("L1", 1)
-        need("t", "eL2", "gL2")
-        wrap("L3", "QA", "ZN", "RL2")
-        hsum("M1", 2)
-        evac("L3", "QA")
-        pick_x("L3")
-        need("t", "eM2", "gM2")
-        wrap("M3", "QB", "ZP", "RM2")
-        evac("M3", "QB")
-        need("v", "dx", "eM3")
-        done(V.tensor_copy(T.XM3[:], T.X[:].indirect(T.M3[:])), "sM3")
-        done(V.tensor_tensor(T.PK[:], T.NF[:], pb[:], A.mult), "vpk")
-        if a == 0:
-            frame_selectors()
-        else:
+                    done(V.tensor_scalar(T.DG[:, (7 * o + d) * 128:(7 * o + d) * 128 + 128], ident, T.WR[:, 8 * o + d:8 * o + d + 1], None, A.mult), "vdg")
+            pick_p("L2")
+            evac("M2", "QB")
+            pick_p("M2")
+            pick_x("M2")
+            need("t", "sdg", "sdg2", "vdg")
+            hsum("L0", 0)
+            hsum("L1", 1)
+            need("t", "eL2", "gL2")
+            wrap("L3", "QA", "ZN", "RL2")
+            hsum("M1", 2)
+            evac("L3", "QA")
+            pick_x("L3")
+            need("t", "eM2", "gM2")
+            wrap("M3", "QB", "ZP", "RM2")
+            done(V.tensor_copy(T.PV[:], T.QT[:, PRVC:PRVC + 128]), "vpv")
+            for q in range(4):
+                done(V.tensor_scalar(T.RW4[:, 128 * q:128 * q + 128], T.QT[:, RWC:RWC + 128], 0.0625, None, A.mult), "vrw4")
+            hsum("L2", 3)
             rewards()
+            evac("M3", "QB")
+            pick_x("M3", "v")
+            need("s", "vpv")
+            done(S.activation(T.XT1[:], T.X[:].indirect(T.PV[:]), COPY), "st1")
+            need("s", "st1")
+            done(S.activation(T.XT2[:], T.XT1[:].indirect(T.PV[:]), COPY), "st2")
+            done(V.tensor_tensor(T.PK[:], T.NF[:], pb[:], A.mult), "vpk")
+            hsum("M2", 4)
+            hsum("M3", 5)
+            hsum("L3", 6)
+        else:
+            need("s", "st1", "st2")
+            pick_x("M1", "s", "XT1", "L0")
+            pick_x("M2", "s", "XT2", "L0")
+            serve(a)
+            hsum("L0", 0)
+            need("t", "eL1", "gL1")
+            wrap("L2", "QA", "ZN", "RL1")
+            hsum("M1", 1)
+            evac("L2", "QA")
+            evac("M1", "QB")
+            pick_x("M3", "s", "XT2", "M1")
+            pick_x("L1", "s")
+            pick_p("L2")
+            pick_x("L2", "v")
+            hsum("M2", 2)
+            need("t", "eL2", "gL2")
+            wrap("L3", "QA", "ZN", "RL2")
+            rewards()
+            evac("L3", "QA")
+            pick_x("L3", "v")
+            done(V.tensor_tensor(T.PK[:], T.NF[:], pb[:], A.mult), "vpk")
+            hsum("M3", 3)
+            hsum("L2", 4)
+            hsum("L1", 5)
+            hsum("L3", 6)
         need("v", "vpk")
         done(V.tensor_scalar(T.KEEP[:], T.PK[:], 1.0, None, A.max), "vkeep")
-        hsum("L2", 3)
-        hsum("M2", 4)
-        hsum("M3", 5)
-        hsum("L3", 6)
-        if a == 0:
-            rewards()
         for q in [rank] + others:
             need("v", "ph%d" % q, "gV" if q == rank else "vr%d_%d" % (a, q))
-            src = VS if q == rank else VR
-            done(V.tensor_tensor(T.PROD[:, 256 * q:256 * q + 256], src[:, 256 * q:256 * q + 256], T["H%d" % q][:, 0:256], A.mult), "vpr")
-        need("t", "vpr", "ves")
+            src = VS[:, 256 * place(core, core):256 * place(core, core) + 256] if q == rank else VR[:, 256 * q:256 * q + 256]
+            done(V.tensor_tensor(T.PROD[:, 256 * q:256 * q + 256], src, T["H%d" % q][:, 0:256], A.mult), "vpr")
+        need("t", "vpr")
         esum("ES", "PROD", True)
         need("v", "pE")
-        done(V.tensor_tensor(T.EM[:], T.M4[:], T.QE[:], A.mult), "vem")
+        done(V.tensor_tensor(T.EM[:], T.M4[:, 0:256], T.QE[:, 0:256], A.mult), "vem")
+        done(V.tensor_tensor(T.QA[:, 0:256], T.M4[:, 256:512], T.QE[:, 256:512], A.mult), "vem")
         need("v", "vem")
-        done(V.tensor_tensor(T.EA[:], T.EM[:, 0:256], T.EM[:, 256:512], A.add), "va1")
+        done(V.tensor_tensor(T.QB[:, 0:128], T.EM[:, 128:256], T.QA[:, 128:256], A.add), "va1")
+        done(V.tensor_tensor(T.EA[:], T.EM[:, 0:128], T.QA[:, 0:128], A.add), "va1")
         need("v", "va1")
-        done(V.tensor_tensor(T.EB[:], T.EA[:, 0:128], T.EA[:, 128:256], A.add), "va2")
-        need("s", "va2")
-        done(S.activation(T.AB[:], T.EB[:], ABS, scale=0.0625), "sab")
-        need("v", "sab", "vkeep")
+        done(V.tensor_tensor(T.EB[:], T.EA[:], T.QB[:, 0:128], A.add), "va2")
+        if a == 0:
+            need("v", "va2")
+            done(V.tensor_scalar(T.EC[:], T.EB[:], -1.0, None, A.mult), "va3")
+            need("v", "va3")
+            done(V.tensor_tensor(T.AB[:], T.EB[:], T.EC[:], A.max), "vab")
+        else:
+            need("s", "va2")
+            done(S.activation(T.AB[:], T.EB[:], ABS), "vab")
+        need("v", "vab", "vkeep")
         done(V.tensor_scalar(T.NI[:], T.AB[:], 0.46875, 63.0, A.subtract, A.min), "vni")
         need("v", "vni")
         done(V.tensor_tensor((T.YO if a else T.PB1)[:], T.NI[:], T.KEEP[:], A.max), "vP")

from concourse.bass import DstId, RemoteDMATransfer
from concourse.mybir import dt, AluOpType, AxisListType, ActivationFunctionType

F16, BF, F32, I32, U16 = "float16", "bfloat16", "float32", "int32", "uint16"
LISTS = ["L0", "L1", "M1", "L2", "M2", "L3", "M3"]
SCRATCH = {
    "PRI": ("sbuf", [128, 128], I32), "PB0": ("sbuf", [128, 128], BF), "PB1": ("sbuf", [128, 128], BF),
    "TI": ("sbuf", [128, 16, 32], I32), "TX": ("sbuf", [128, 16, 32], F16), "TT": ("sbuf", [128, 16, 32], F16),
    "X": ("sbuf", [128, 2048], BF), "VALB": ("sbuf", [128, 4096], BF), "PW": ("sbuf", [128, 2048], I32),
    "IM": ("sbuf", [128, 160], I32), "I16": ("sbuf", [128, 128], I32), "KP": ("sbuf", [128, 1], I32), "T8I": ("sbuf", [128, 64], I32),
    "CI": ("sbuf", [128, 8], I32), "CF": ("sbuf", [128, 8], F32), "CG": ("sbuf", [128, 8], F32),
    "BO": ("sbuf", [128, 128], BF), "TM": ("sbuf", [128, 128], BF), "IDW": ("sbuf", [128, 160], BF), "ONB": ("sbuf", [128, 144], BF),
    "C16": ("sbuf", [128, 128], BF), "PM": ("sbuf", [128, 512], BF), "Z2": ("sbuf", [128, 144], F16), "Z2T": ("sbuf", [128, 144], F16),
    "ZN": ("sbuf", [128, 144], BF), "ZP": ("sbuf", [128, 144], BF), "ES": ("sbuf", [128, 256], BF), "ER": ("sbuf", [128, 256], BF),
    "T8H": ("sbuf", [128, 64], F16), "PV": ("sbuf", [128, 128], U16),
    "ONE": ("sbuf", [128, 128], F32), "CS": ("sbuf", [128, 128], F32), "SI": ("sbuf", [128, 128], I32), "RI": ("sbuf", [128, 128], I32),
    "K2": ("sbuf", [128, 128], I32), "NF": ("sbuf", [128, 128], F32), "CODE": ("sbuf", [128, 128], F16), "M4": ("sbuf", [128, 512], F16),
    "MK": ("sbuf", [128, 512], F16), "MN": ("sbuf", [128, 512], F16), "MP": ("sbuf", [128, 512], F16), "RW4": ("sbuf", [128, 512], F16),
    "KS0": ("sbuf", [128, 64], U16), "KS1": ("sbuf", [128, 64], U16), "KL0": ("sbuf", [128, 64], U16), "KL1": ("sbuf", [128, 64], U16),
    "VS0": ("sbuf", [128, 1024], BF), "VS1": ("sbuf", [128, 1024], BF), "VR0": ("sbuf", [128, 1024], BF), "VR1": ("sbuf", [128, 1024], BF),
    "PROD": ("sbuf", [128, 1024], F16), "EM": ("sbuf", [128, 256], F32), "EA": ("sbuf", [128, 128], F32), "EB": ("sbuf", [128, 128], F32),
    "EC": ("sbuf", [128, 128], F32), "AB": ("sbuf", [128, 128], F32), "NI": ("sbuf", [128, 128], I32), "PK": ("sbuf", [128, 128], F32),
    "KEEP": ("sbuf", [128, 128], F32), "YO": ("sbuf", [128, 128], F32), "WS": ("sbuf", [128, 7], BF), "WF": ("sbuf", [128, 7], F32),
    "WR": ("sbuf", [128, 32], BF), "WG": ("sbuf", [128, 32], F32), "DG": ("sbuf", [128, 28 * 128], BF),
    "QA": ("psum", [128, 512], F32), "QB": ("psum", [128, 512], F32), "QT": ("psum", [128, 512], F32), "QE": ("psum", [128, 512], F32),
    "XT1": ("sbuf", [128, 2048], BF), "XT2": ("sbuf", [128, 2048], BF),
}
for _n in LISTS:
    SCRATCH[_n] = ("sbuf", [128, 64], U16)
    SCRATCH["X" + _n] = ("sbuf", [128, 1024], BF)
for _n in LISTS[1:5]:
    SCRATCH["R" + _n] = ("sbuf", [128, 1024], F16)
for _q in range(4):
    SCRATCH["H%d" % _q] = ("psum", [128, 512], F32)
SEMAPHORES = (["dpri", "dtab", "dw", "dx", "dval", "dpw", "dy", "gi", "gz", "gsel", "ges", "ges2", "vz", "vcon", "vc", "vc2", "vc3", "vi8", "vbo", "vtm",
               "vtm2", "vpb", "sperm", "vcv", "vtr", "vz4", "vone", "vid", "vpv", "vscan", "vS", "vr", "vnf", "vcode", "vm0", "vm1", "vm2", "vm3",
               "vmk", "vmn", "vmp", "vpk", "vkeep", "eK", "eO", "gV", "gU", "vrw4", "vdg", "vpr", "vem", "va1", "va2", "va3", "vab", "vni", "vP", "ptab",
               "pA", "pB", "pK", "ph0", "ph1", "ph2", "ph3", "pE", "swf", "sdg", "swg", "sdg2", "st1", "st2", "wl", "wr", "kl", "vl",
               "kr0", "kr1", "ko0", "ko1"]
              + ["e" + n for n in LISTS] + ["p" + n for n in LISTS] + ["s" + n for n in LISTS] + ["g" + n for n in LISTS[1:5]]
              + ["vr%d_%d" % (a, q) for a in range(2) for q in range(4)])


def rank_program(g, core, T, topo):
    rank = T.rank_of(core)
    if rank is None:
        return
    A = AluOpType
    COPY, ABS = ActivationFunctionType.Copy, ActivationFunctionType.Abs
    V, S, P = g.vector, g.scalar, g.tensor
    Q = {"v": V, "s": S, "t": P, "y": g.sync, "g": g}
    tot, got = {}, {}

    def done(ins, name, n=1):
        ins.then_inc(T.sem[name], n)
        tot[name] = tot.get(name, 0) + n

    def need(q, *names):
        for n in names:
            if got.get((q, n), 0) < tot[n]:
                Q[q].wait_ge(T.sem[n], tot[n])
                got[(q, n)] = tot[n]

    def off_of(src):
        return [c for c in T.cores if c not in topo.cores_of(src)]

    def on_of(src):
        return [c for c in T.cores if c != src and c in topo.cores_of(src)]

    def engines_of(src):
        off, out = off_of(src), {}
        eo = topo.engines(src, off[0])
        n = len(eo) // len(off)
        for k, c in enumerate(off):
            out[c] = eo[k * n:(k + 1) * n]
        for c in on_of(src):
            out[c] = [e for e in topo.engines(src, c) if e not in eo]
        return out

    def place(c, at):
        return (off_of(at) + on_of(at) + [at]).index(c)

    off, on = off_of(core), on_of(core)
    peers = on + off
    others = [T.rank_of(c) for c in peers]
    half = len(off)
    eng = engines_of(core)
    inc = {c: len(engines_of(c)[core]) for c in peers}

    def send(to, src_of, dst_of, sem_of, local):
        tr = []
        for c in to:
            rid, pid = topo.addr(c, core)
            m = 0
            for e in eng[c]:
                m |= 1 << e
            tr.append(RemoteDMATransfer(dst_ids=[DstId(rid=rid, pnc=pid)], dma_engine_mask=m, remote_sem=sem_of(c), src=src_of(c), dst=dst_of(c)))
        g.remote_dma_fused(tr, local_sem=T.sem[local])
        tot[local] = tot.get(local, 0) + sum(len(eng[c]) for c in to)

    done(g.sync.dma_start(T.PRI[:], T.pri[:]), "dpri", 16)
    done(S.dma_start(T.WS[:], T.w[:]), "dw", 16)
    done(g.sync.dma_start(T.TI[:, 0:4, :], T.key[:]), "dtab", 16)
    done(S.dma_start(T.TI[:, 4:8, :], T.nxt[:]), "dtab", 16)
    done(g.sync.dma_start(T.TI[:, 8:12, :], T.prv[:]), "dtab", 16)
    done(S.dma_start(T.TI[:, 12:16, :], T.rw[:]), "dtab", 16)
    done(S.dma_start(T.X[:], T.x[:]), "dx", 16)

    done(g.iota(T.IM[:], [[1, 160]], -16, 0), "gi")
    done(g.iota(T.KP[:], [[0, 1]], 0, 1), "gi")
    done(g.iota(T.T8I[:], [[0, 4], [128, 16]], 0, 0), "gi")
    done(g.iota(T.PW[:, 1024:2048], [[0, 1024]], 0, 0), "gz")
    done(V.memset(T.PW[:, 0:1024], 0), "vz")
    need("y", "gz", "vz")
    done(g.sync.dma_start(T.PW[0:128:16, :], T.nxt[:]), "dpw", 16)
    done(g.sync.dma_start(T.PW[1:128:16, :], T.prv[:]), "dpw", 16)
    done(g.sync.dma_start(T.PW[2:128:16, :], T.rw[:]), "dpw", 16)
    done(g.sync.dma_start(T.VALB[:], T.val[:]), "dval", 16)
    need("g", "dw")
    send(peers, lambda c: T.WS[:], lambda c: T.WR[:, 8 * rank:8 * rank + 7], lambda c: T.sem.wr, "wl")
    tot["wr"] = sum(inc.values())

    done(V.memset(T.ONE[:], 1.0), "vone")
    need("v", "gi")
    kp = T.KP[:]
    m = T.IM[:, 16:144]
    ident = T.IDW[:, 16:144]

    def bits(j, sh, msk):
        done(V.tensor_scalar(T.CI[:, j:j + 1], kp, sh, msk, A.logical_shift_right, A.bitwise_and), "vc")

    cf = lambda j: T.CF[:, j:j + 1]
    cg = lambda j: T.CG[:, j:j + 1]
    bits(0, 4, 7)
    bits(1, 4, 1)
    bits(2, 0, 127)
    bits(3, 0, 15)
    bits(4, 0, 7)
    bits(5, 0, 112)
    bits(6, 3, 1)
    done(V.tensor_scalar(T.I16[:], m, 4, None, A.logical_shift_right), "vi8")
    need("v", "vc")
    done(V.tensor_copy(T.CF[:, 0:7], T.CI[:, 0:7]), "vc2")
    need("v", "vc2", "vi8")
    done(V.tensor_scalar(T.BO[:], T.I16[:], cf(0), None, A.is_equal), "vbo")
    done(V.tensor_scalar(T.TM[:], m, cf(2), -1.0, A.is_lt, A.mult), "vtm")
    done(V.tensor_scalar(cg(5), cf(1), 0.0, None, A.is_equal), "vc3")
    done(V.tensor_tensor(cg(1), cf(5), cf(6), A.add), "vc3")
    done(V.tensor_scalar(cg(7), cf(3), 8.0, None, A.mult), "vc3")
    need("v", "vbo", "vtm")
    done(V.tensor_tensor(T.TM[:], T.TM[:], T.BO[:], A.mult), "vtm2")
    done(V.tensor_scalar(T.IDW[:], T.IM[:], cf(2), None, A.is_equal), "vid")
    need("v", "dpri")
    done(V.tensor_copy(T.PB0[:], T.PRI[:]), "vpb")
    need("v", "vc3")
    done(V.tensor_scalar(T.Z2T[:], T.IM[:, 0:144], cg(1), cf(4), A.is_equal, A.mult), "vz4")
    done(V.tensor_scalar(T.Z2[:], T.IM[:, 0:144], cg(1), None, A.is_equal), "vz4")
    done(V.tensor_scalar(T.T8H[:], T.T8I[:], cg(7), None, A.add), "vz4")

    need("s", "vid", "vc3", "vc2")
    for n, (lo, msk) in enumerate([(16, cg(5)), (32, cf(1)), (0, cg(5)), (16, cf(1))]):
        done(S.activation(T.PM[:, 128 * n:128 * n + 128], T.IDW[:, lo:lo + 128], COPY, scale=msk), "sperm")
    need("s", "dw")
    done(S.activation(T.WF[:], T.WS[:], COPY), "swf")
    need("s", "swf")
    for d in range(7):
        o = (7 * rank + d) * 128
        done(S.activation(T.DG[:, o:o + 128], ident, COPY, scale=T.WF[:, d:d + 1]), "sdg")

    def sums(a):
        pb = T.PB0 if a == 0 else T.PB1
        need("t", "vbo", "vpb" if a == 0 else "vP")
        done(P.matmul(T.QA[:, 0:128], T.BO[:], pb[:], True, True), "pA")
        need("t", "vtm2")
        done(P.matmul(T.QB[:, 0:128], T.TM[:], pb[:], True, True), "pB")

    def tables_out():
        need("t", "sperm", "vtr")
        for b1 in range(8):
            bt = b1 % 2
            for ga in range(2):
                n = 2 * ga + bt
                ins = P.matmul(T.QT[:, b1:512:8], T.PM[:, 128 * n:128 * n + 128], T.TT[:, b1 // 2:16:4, 16 * ga:16 * ga + 16], ga == 0, ga == 1)
            if b1 == 7:
                done(ins, "ptab")

    def gpsimd_selectors():
        need("g", "vcon")
        done(g.affine_select(T.ZN[:], T.ONB[:], [[-16, 9], [-1000, 16]], A.is_equal, 0.0, 16, 1), "gsel")
        done(g.affine_select(T.ZP[:], T.ONB[:], [[-16, 9], [-1000, 16]], A.is_equal, 0.0, 15, 1), "gsel")
        for ih in range(2):
            pat, base = [[-16, 8], [1000 if ih else -1000, 2], [0, 8]], -1000 if ih else 0
            o = slice(128 * ih, 128 * ih + 128)
            done(g.affine_select(T.ER[:, o], T.C16[:], pat, A.is_equal, 0.0, base - 2, 1), "ges2")
            done(g.affine_select(T.ES[:, o], T.C16[:], pat, A.is_ge, 0.0, base, 1), "ges")
        need("g", "ges")
        for ih in range(2):
            o = slice(128 * ih, 128 * ih + 128)
            done(g.affine_select(T.ES[:, o], T.ES[:, o], [[16, 8], [0, 2], [0, 8]], A.is_ge, 0.0, 15, -1), "ges2")

    KEYC, NXTC, PRVC, RWC = 0, 128, 256, 384
    STEP = {"L0": 3, "L1": 4, "L2": 5, "L3": 6, "M1": 2, "M2": 1, "M3": 0}
    MASKS = ["vm0", "vm1", "vm2", "vm3"]

    def blocksum(name, bank, sel, rows, first=True):
        for cl in range(8):
            ins = P.matmul(T[bank][:, 0:64], T[sel][:, 16 - 2 * cl:144 - 2 * cl], T[rows][:, cl:512:8], first and cl == 0, cl == 7)
        done(ins, name)

    def wrap(lst, bank, sel, rows):
        need("t", "gsel")
        for ro in range(16):
            ins = P.matmul(T[bank][:, 0:64], T[sel][:, 16 - ro:144 - ro], T[rows][:, ro:1024:16], ro == 0, ro == 15)
        done(ins, "p" + lst)

    def evac(lst, bank):
        need("v", "p" + lst)
        done(V.tensor_copy(T[lst][:], T[bank][:, 0:64]), "e" + lst)

    def mul(out, col, sem, qs=range(4)):
        for q in qs:
            need("v", MASKS[q])
            done(V.tensor_tensor(T[out][:, 128 * q:128 * q + 128], T.M4[:, 128 * q:128 * q + 128], T.QT[:, col:col + 128], A.mult), sem)

    def pick_x(lst, on_q="s", table="X", at=None):
        at = at or lst
        need(on_q, "dx", "e" + at)
        src = T[table][:].indirect(T[at][:])
        if on_q == "s":
            done(S.activation(T["X" + lst][:], src, COPY), "s" + lst)
        else:
            done(V.tensor_copy(T["X" + lst][:], src), "s" + lst)

    def pick_p(lst):
        need("v", "dpw", "e" + lst)
        done(V.tensor_copy(T["R" + lst][:], T.PW[:].indirect(T[lst][:])), "g" + lst)

    def hsum(lst, k):
        need("t", "s" + lst)
        for q in [rank] + others:
            o = (7 * q + STEP[lst]) * 128
            ins = P.matmul(T["H%d" % q][:, 0:256], T.DG[:, o:o + 128], T["X" + lst][:, 256 * q:256 * q + 256], k == 0, k == 6)
            if k == 6:
                done(ins, "ph%d" % q)

    def esum(sel, rows, last):
        for ih in range(2):
            ins = P.matmul(T.QE[:], T[sel][:, 128 * ih:128 * ih + 128], T[rows][:, ih:1024:2], False, last and ih == 1)
        if last:
            done(ins, "pE")

    def rewards():
        need("t", "vrw4", "ges2")
        P.matmul(T.QE[:], ident, T.RW4[:], True, False)
        esum("ER", "RL1", False)
        esum("ER", "RL2", False)

    def serve(a):
        KL, VS, VR = T["KL%d" % a], T["VS%d" % a], T["VR%d" % a]
        src = lambda c: VS[:, 256 * place(c, core):256 * place(c, core) + 256]
        dst = lambda c: VR[:, 256 * rank:256 * rank + 256]
        sem = lambda c: T.sem["vr%d_%d" % (a, rank)]
        need("s", "dval", "ko%d" % a)
        done(S.activation(VS[:, 0:256 * half], T.VALB[:].indirect(KL[:, 0:16 * half]), COPY), "gU")
        need("s", "kr%d" % a, "eO")
        done(S.activation(VS[:, 256 * half:1024], T.VALB[:].indirect(KL[:, 16 * half:64]), COPY), "gV")
        need("g", "gU")
        send(off, src, dst, sem, "vl")
        need("g", "gV")
        send(on, src, dst, sem, "vl")
        for c in peers:
            tot["vr%d_%d" % (a, T.rank_of(c))] = inc[c]

    for a in range(2):
        pb = T.PB0 if a == 0 else T.PB1
        KS, KL, VS, VR = T["KS%d" % a], T["KL%d" % a], T["VS%d" % a], T["VR%d" % a]
        sums(a)
        need("v", "pA", "vone")
        done(V.tensor_tensor_scan(T.CS[:], T.ONE[:], T.QA[:, 0:128], 0.0, A.mult, A.add), "vscan")
        need("v", "pB", "vscan")
        done(V.tensor_tensor(T.SI[:], T.CS[:], T.QB[:, 0:128], A.add), "vS")
        need("v", "vS")
        done(V.tensor_scalar(T.RI[:], T.SI[:], 127, None, A.bitwise_and), "vr")
        done(V.tensor_scalar(T.K2[:], T.SI[:], 6, 6, A.arith_shift_right, A.bitwise_and), "vr")
        if a == 0:
            need("v", "dtab")
            done(V.tensor_scalar(T.TX[:, 0:4, :], T.TI[:, 0:4, :], 2048.0, None, A.subtract), "vcv")
            done(V.tensor_copy(T.TX[:, 4:16, :], T.TI[:, 4:16, :]), "vcv")
        need("v", "vr")
        done(V.tensor_tensor(T.NF[:], T.RI[:], pb[:], A.is_ge), "vnf")
        if a == 0:
            need("v", "vcv")
            done(V.transpose(T.TT[:], T.TX[:]), "vtr")
            tables_out()
        need("v", "vnf")
        done(V.tensor_tensor(T.CODE[:], T.K2[:], T.NF[:], A.add), "vcode")
        need("v", "vcode")
        for q in range(4):
            done(V.tensor_scalar(T.M4[:, 128 * q:128 * q + 128], T.CODE[:], float(2 * ((q + 1) % 4)), None, A.is_equal), MASKS[q])
        need("t", "vz4", "vid", "vscan", *MASKS)
        P.matmul(T.QA[:, 0:64], ident, T.T8H[:], True, False)
        blocksum("pL0", "QA", "Z2T", "M4", False)
        need("v", "ptab")
        mul("MK", KEYC, "vmk")
        need("t", "vmk", "vS")
        blocksum("pK", "QB", "Z2", "MK")
        evac("L0", "QA")
        pick_x("L0")
        mul("MN", NXTC, "vmn", (0, 1))
        need("v", "pK")
        done(V.tensor_scalar(KS[:], T.QB[:, 0:64], 2048.0, None, A.add), "eK")
        need("g", "eK")
        send(peers, lambda c: KS[:, 16 * T.rank_of(c):16 * T.rank_of(c) + 16], lambda c: KL[:, 16 * place(core, c):16 * place(core, c) + 16],
             lambda c: T.sem[("ko%d" if c in off else "kr%d") % a], "kl")
        tot["ko%d" % a] = sum(inc[c] for c in off)
        tot["kr%d" % a] = sum(inc[c] for c in on)
        mul("MN", NXTC, "vmn", (2, 3))
        need("t", "vmn", "eL0")
        blocksum("pL1", "QA", "Z2", "MN")
        mine = 16 * place(core, core)
        done(V.tensor_scalar(KL[:, mine:mine + 16], T.QB[:, 16 * rank:16 * rank + 16], 2048.0, None, A.add), "eO")
        if a == 0:
            done(V.memset(T.ONB[:], 1.0), "vcon")
            done(V.memset(T.C16[:], 0.0625), "vcon")
            gpsimd_selectors()
        mul("MP", PRVC, "vmp")
        need("t", "vmp", "eK", "eO")
        blocksum("pM1", "QB", "Z2", "MP")
        evac("L1", "QA")
        pick_p("L1")
        if a == 0:
            evac("M1", "QB")
            pick_p("M1")
            need("t", "eL1", "gL1")
            wrap("L2", "QA", "ZN", "RL1")
            need("s", "wr")
            o = others[0]
            done(S.activation(T.WG[:, 0:7], T.WR[:, 8 * o:8 * o + 7], COPY), "swg")
            need("s", "swg")
            for d in range(7):
                done(S.activation(T.DG[:, (7 * o + d) * 128:(7 * o + d) * 128 + 128], ident, COPY, scale=T.WG[:, d:d + 1]), "sdg2")
            pick_x("L1")
            pick_x("M1")
            serve(a)
            evac("L2", "QA")
            pick_x("L2")
            need("t", "eM1", "gM1")
            wrap("M2", "QB", "ZP", "RM1")
            need("v", "wr")
            for o in others[1:]:
                for d in range(7):
                    done(V.tensor_scalar(T.DG[:, (7 * o + d) * 128:(7 * o + d) * 128 + 128], ident, T.WR[:, 8 * o + d:8 * o + d + 1], None, A.mult), "vdg")
            pick_p("L2")
            evac("M2", "QB")
            pick_p("M2")
            pick_x("M2")
            need("t", "sdg", "sdg2", "vdg")
            hsum("L0", 0)
            hsum("L1", 1)
            need("t", "eL2", "gL2")
            wrap("L3", "QA", "ZN", "RL2")
            hsum("M1", 2)
            evac("L3", "QA")
            pick_x("L3")
            need("t", "eM2", "gM2")
            wrap("M3", "QB", "ZP", "RM2")
            done(V.tensor_copy(T.PV[:], T.QT[:, PRVC:PRVC + 128]), "vpv")
            for q in range(4):
                done(V.tensor_scalar(T.RW4[:, 128 * q:128 * q + 128], T.QT[:, RWC:RWC + 128], 0.0625, None, A.mult), "vrw4")
            hsum("L2", 3)
            rewards()
            evac("M3", "QB")
            pick_x("M3", "v")
            need("s", "vpv")
            done(S.activation(T.XT1[:], T.X[:].indirect(T.PV[:]), COPY), "st1")
            need("s", "st1")
            done(S.activation(T.XT2[:], T.XT1[:].indirect(T.PV[:]), COPY), "st2")
            done(V.tensor_tensor(T.PK[:], T.NF[:], pb[:], A.mult), "vpk")
            hsum("M2", 4)
            hsum("M3", 5)
            hsum("L3", 6)
        else:
            need("s", "st1", "st2")
            pick_x("M1", "s", "XT1", "L0")
            pick_x("M2", "s", "XT2", "L0")
            serve(a)
            hsum("L0", 0)
            need("t", "eL1", "gL1")
            wrap("L2", "QA", "ZN", "RL1")
            hsum("M1", 1)
            evac("L2", "QA")
            evac("M1", "QB")
            pick_x("M3", "s", "XT2", "M1")
            pick_x("L1", "s")
            pick_p("L2")
            pick_x("L2", "v")
            hsum("M2", 2)
            need("t", "eL2", "gL2")
            wrap("L3", "QA", "ZN", "RL2")
            rewards()
            evac("L3", "QA")
            pick_x("L3", "v")
            done(V.tensor_tensor(T.PK[:], T.NF[:], pb[:], A.mult), "vpk")
            hsum("M3", 3)
            hsum("L2", 4)
            hsum("L1", 5)
            hsum("L3", 6)
        need("v", "vpk")
        done(V.tensor_scalar(T.KEEP[:], T.PK[:], 1.0, None, A.max), "vkeep")
        for q in [rank] + others:
            need("v", "ph%d" % q, "gV" if q == rank else "vr%d_%d" % (a, q))
            src = VS[:, 256 * place(core, core):256 * place(core, core) + 256] if q == rank else VR[:, 256 * q:256 * q + 256]
            done(V.tensor_tensor(T.PROD[:, 256 * q:256 * q + 256], src, T["H%d" % q][:, 0:256], A.mult), "vpr")
        need("t", "vpr")
        esum("ES", "PROD", True)
        need("v", "pE")
        done(V.tensor_tensor(T.EM[:], T.M4[:, 0:256], T.QE[:, 0:256], A.mult), "vem")
        done(V.tensor_tensor(T.QA[:, 0:256], T.M4[:, 256:512], T.QE[:, 256:512], A.mult), "vem")
        need("v", "vem")
        done(V.tensor_tensor(T.QB[:, 0:128], T.EM[:, 128:256], T.QA[:, 128:256], A.add), "va1")
        done(V.tensor_tensor(T.EA[:], T.EM[:, 0:128], T.QA[:, 0:128], A.add), "va1")
        need("v", "va1")
        done(V.tensor_tensor(T.EB[:], T.EA[:], T.QB[:, 0:128], A.add), "va2")
        if a == 0:
            need("v", "va2")
            done(V.tensor_scalar(T.EC[:], T.EB[:], -1.0, None, A.mult), "va3")
            need("v", "va3")
            done(V.tensor_tensor(T.AB[:], T.EB[:], T.EC[:], A.max), "vab")
        else:
            need("s", "va2")
            done(S.activation(T.AB[:], T.EB[:], ABS), "vab")
        need("v", "vab", "vkeep")
        done(V.tensor_scalar(T.NI[:], T.AB[:], 0.46875, 63.0, A.subtract, A.min), "vni")
        need("v", "vni")
        done(V.tensor_tensor((T.YO if a else T.PB1)[:], T.NI[:], T.KEEP[:], A.max), "vP")
    need("y", "vP")
    done(g.sync.dma_start(T.y[:], T.YO[:]), "dy", 16)
    need("y", "dy")
    for n in sorted(tot):
        if max([got.get((q, n), 0) for q in Q]) < tot[n]:
            need("g", n)
